import numpy as np
import ml_dtypes


def mxq(x, axis, fmt="e4m3"):
    dtype, down = {"e4m3": (ml_dtypes.float8_e4m3fn, 7), "e5m2": (ml_dtypes.float8_e5m2, 14)}[fmt]
    v = np.moveaxis(np.asarray(x, np.float32).astype(ml_dtypes.bfloat16).astype(np.float64), axis, -1)
    blocks = v.reshape(v.shape[:-1] + (-1, 32))
    amax = np.abs(blocks).max(-1, keepdims=True)
    byte = np.maximum(np.where(amax > 0, np.frexp(amax)[1] - 1 + 127, 0) - down, 1)
    scale = np.exp2(byte - 127.0)
    codes = (blocks / scale).astype(np.float32).astype(dtype).astype(np.float64)
    return np.moveaxis((codes * scale).reshape(v.shape), -1, axis)


WIDE = False


def mx_kscale(k):
    if not WIDE:
        return np.ones(k)
    levels = np.array([10, -10, 5, -5, 0])
    if k % 512:
        return np.exp2(np.random.permutation(np.resize(levels, k // 32))).repeat(32)
    a = np.empty((k // 512, 16))
    for p in range(k // 512):
        a[p, :8] = np.random.permutation(np.resize(levels, 8))
        for g in range(8):
            far = levels[np.abs(levels - a[p, g]) >= 10]
            a[p, g + 8] = far[np.random.randint(len(far))]
    return np.exp2(a.ravel()).repeat(32)


def f64(x):
    return np.asarray(x).astype(np.float64)


def striped8(idx):
    return np.asarray(idx).reshape(8, -1, 16).transpose(0, 2, 1).reshape(128, -1).astype(np.uint16)


def unstriped8(offs):
    return offs.reshape(8, 16, -1).transpose(0, 2, 1).reshape(8, -1).astype(np.int64)


def pick8(x, idx, run):
    r = np.arange(len(x))
    return x[r[:, None], idx[r % (8 * run) // run]]


E2M1 = np.array([0.0, 0.5, 1.0, 1.5, 2.0, 3.0, 4.0, 6.0, -0.0, -0.5, -1.0, -1.5, -2.0, -3.0, -4.0, -6.0])


def pack_weight(w, fmt):
    k, n = w.shape
    w = f64(np.asarray(w, np.float32).astype(ml_dtypes.bfloat16)).reshape(k // 32, 32, n)
    amax = np.abs(w).max(1)
    if fmt == "e4m3":
        byte = np.frexp(amax)[1] - 1 + 127 - 7
    else:
        mant, ex = np.frexp(amax / 6.0)
        byte = np.where(mant > 0.5, ex, ex - 1) + 127
    byte = np.clip(np.where(amax > 0, byte, 1), 1, 254)
    scaled = (w * np.exp2(127.0 - byte)[:, None, :]).reshape(k, n).astype(np.float32)
    by_word = np.ascontiguousarray(scaled.reshape(k // 512, 128, 4, n).transpose(0, 1, 3, 2))
    if fmt == "e4m3":
        words = by_word.astype(ml_dtypes.float8_e4m3fn).view(np.uint8)
    else:
        c = by_word.astype(ml_dtypes.float4_e2m1fn).view(np.uint8) & 0xF
        words = (c[..., 0::2] | (c[..., 1::2] << 4)).reshape(k // 512, 128, 2 * n)
    return np.ascontiguousarray(words), np.ascontiguousarray(byte.astype(np.uint8).reshape(k // 512, 16, n))


def unpack_weight(words, scales, fmt):
    g, _, n = scales.shape
    words = np.ascontiguousarray(words).reshape(g, 128, n, -1)
    if fmt == "e4m3":
        vals = words.view(ml_dtypes.float8_e4m3fn).astype(np.float64)
    else:
        nib = np.empty((g, 128, n, 4), np.uint8)
        nib[..., 0::2] = words & 0xF
        nib[..., 1::2] = words >> 4
        vals = E2M1[nib]
    vals = vals * np.repeat(np.exp2(scales.astype(np.float64) - 127.0), 8, axis=1)[..., None]
    return vals.transpose(0, 1, 3, 2).reshape(g * 512, n)


K, T, D, I, Q = 512, 1024, 512, 512, 128


def setup_inputs():
    n = np.random.standard_normal
    idx = np.stack([np.random.permutation(T)[:I] for _ in range(8)])
    fk = mx_kscale(K)
    fd = mx_kscale(D)
    embp = pack_weight(n((K, T)) / fk[:, None], "e4m3")
    return {
        "emb_words": embp[0],
        "emb_scales": embp[1],
        "wk": (n((K, D)) * 1 / np.sqrt(K) * fk[:, None] / fd).astype(np.float32),
        "query": (n((D, Q)) * 0.8 / np.sqrt(D) * fd[:, None]).astype(np.float32),
        "offs": striped8(idx),
    }


def reference(emb_words, emb_scales, wk, query, offs):
    idx = unstriped8(offs)
    embu = unpack_weight(emb_words, emb_scales, "e4m3")
    wkq = mxq(f64(wk), 0, "e4m3")
    key = wkq.T @ embu
    queryq = mxq(f64(query), 0, "e4m3")
    keyidxq = mxq(pick8(key, idx, 64), 0, "e4m3")
    a = queryq.T @ keyidxq
    p = np.exp(a - np.max(a, axis=1, keepdims=True))
    y = p / np.sum(p, axis=1, keepdims=True) * 512.0
    return y

@@ -1,0 +1,172 @@
+from contextlib import ExitStack
+
+import concourse.mybir as mybir
+
+K, T, D, I, Q = 512, 1024, 512, 512, 128
+FLOPS = 2 * K * D * T + 2 * D * Q * I
+
+F32 = mybir.dt.float32
+BF16 = mybir.dt.bfloat16
+I32 = mybir.dt.int32
+U32 = mybir.dt.uint32
+U16 = mybir.dt.uint16
+U8 = mybir.dt.uint8
+FP8X4 = mybir.dt.float8_e4m3fn_x4
+ALU = mybir.AluOpType
+EXP = mybir.ActivationFunctionType.Exp
+
+P = 128
+PACK = 4
+BANK = 512
+HALF = I // 2
+
+
+def tile_attend_grouppick_fresh_kernel(tc, emb_words, emb_scales, wk, query, offs, out):
+    nc = tc.nc
+    with ExitStack() as ctx:
+        sb = ctx.enter_context(tc.tile_pool(name="sb", bufs=1))
+        key_ps = ctx.enter_context(tc.psum_pool(name="key_ps", bufs=6))
+        score_ps = ctx.enter_context(tc.psum_pool(name="score_ps", bufs=2))
+
+        offsets = sb.tile([P, I // 16], U16, name="offsets")
+
+        emb_sc = sb.tile([P, T], U8, name="emb_sc", align_bytes=64)
+        nc.vector.memset(emb_sc[:].bitcast(I32), 0)
+        for g in range(4):
+            nc.scalar.dma_start(
+                out=emb_sc[32 * g : 32 * g + 4, :].bitcast(I32),
+                in_=emb_scales[0, 4 * g : 4 * g + 4, :].bitcast(I32),
+            )
+
+        wk_rows = wk.rearrange("(p t) d -> p t d", t=PACK)
+        wk_raw = []
+        for c in range(2):
+            raw = sb.tile([P, PACK, D // 2], F32, name="wk_raw%d" % c)
+            nc.sync.dma_start(out=raw[:], in_=wk_rows[:, :, c * (D // 2) : (c + 1) * (D // 2)])
+            wk_raw.append(raw)
+
+        emb_bytes = emb_words[0].rearrange("p n t -> p (n t)")
+        emb_codes = []
+        for h in range(2):
+            codes = sb.tile([P, BANK], U32, name="emb_codes%d" % h, align_bytes=64)
+            nc.sync.dma_start(
+                out=codes[:].bitcast(I32),
+                in_=emb_bytes[:, h * BANK * PACK : (h + 1) * BANK * PACK].bitcast(I32),
+            )
+            emb_codes.append(codes)
+
+        nc.sync.dma_start(offsets[:], offs)
+
+        q_raw = sb.tile([P, PACK, Q], F32, name="q_raw")
+        q_planes = query.rearrange("(b j r) q -> j b r q", j=PACK, r=8)
+        for j in range(PACK):
+            nc.sync.dma_start(out=q_raw[:, j, :], in_=q_planes[j])
+
+        warm_in = sb.tile([P, 1], F32, name="warm_in")
+        warm_out = sb.tile([P, 1], F32, name="warm_out")
+        nc.vector.memset(warm_in[:], 0.0)
+        nc.scalar.activation(warm_out[:], warm_in[:], EXP)
+
+        wk_bf = [sb.tile([P, P * PACK], BF16, name="wk_bf%d" % j, align_bytes=64) for j in range(PACK)]
+        for c in range(2):
+            src = wk_raw[c][:].rearrange("p t (b j h i) -> p j b h t i", j=PACK, h=2, i=4)
+            for j in range(PACK):
+                dst = wk_bf[j][:].rearrange("p (c b h i t) -> p c b h t i", c=2, h=2, i=4, t=PACK)
+                if j < 2:
+                    nc.vector.tensor_copy(out=dst[:, c], in_=src[:, j])
+                else:
+                    nc.scalar.copy(out=dst[:, c], in_=src[:, j])
+
+        keys = []
+        for j in range(PACK):
+            wk_codes = sb.tile([P, P], U32, name="wk_codes%d" % j, tag="stationary%d" % j, align_bytes=64)
+            wk_sc = sb.tile([P, P], U8, name="wk_sc%d" % j, align_bytes=64)
+            nc.vector.quantize_mx(out=wk_codes[:].bitcast(FP8X4), scales=wk_sc[:], in_=wk_bf[j][:])
+            key = sb.tile([P, T], F32, name="key%d" % j)
+            cuts = (0, BANK, BANK + BANK // 2, T) if j == 0 else (0, BANK, T)
+            for a, b in zip(cuts, cuts[1:]):
+                h = a // BANK
+                bank = key_ps.tile([P, b - a], F32, name="key_bank")
+                nc.tensor.matmul_mx(
+                    out=bank[:],
+                    lhsT=wk_codes[:].bitcast(FP8X4),
+                    lhsT_scale=wk_sc[:],
+                    rhs=emb_codes[h][:, a - h * BANK : b - h * BANK].bitcast(FP8X4),
+                    rhs_scale=emb_sc[:, a:b],
+                    start=True,
+                    stop=True,
+                )
+                if j == 0 and a == BANK:
+                    nc.vector.tensor_copy(out=key[:, a:b], in_=bank[:])
+                else:
+                    nc.scalar.copy(out=key[:, a:b], in_=bank[:])
+            keys.append(key)
+
+        q_bf = sb.tile([P, Q * PACK], BF16, name="q_bf", tag="stationary%d" % (PACK - 1), align_bytes=64)
+        nc.scalar.copy(
+            out=q_bf[:].rearrange("p (c i t) -> p c t i", i=4, t=PACK),
+            in_=q_raw[:].rearrange("p t (c i) -> p c t i", i=4),
+        )
+
+        picked = [sb.tile([P, PACK, HALF], BF16, name="picked%d" % h) for h in range(2)]
+        for j in range(PACK):
+            for h in range(2):
+                nc.vector.tensor_copy(
+                    out=picked[h][:, j, :],
+                    in_=keys[j][:].indirect(offsets[:, h * (HALF // 16) : (h + 1) * (HALF // 16)]),
+                )
+
+        q_codes = sb.tile([P, Q], U32, name="q_codes", align_bytes=64)
+        q_sc = sb.tile([P, Q], U8, name="q_sc", align_bytes=64)
+        nc.vector.quantize_mx(out=q_codes[:].bitcast(FP8X4), scales=q_sc[:], in_=q_bf[:])
+
+        picked_bf = []
+        for h in range(2):
+            woven = sb.tile([P, HALF * PACK], BF16, name="woven%d" % h, align_bytes=64)
+            dst = woven[:].rearrange("p (c i t) -> p c t i", i=4, t=PACK)
+            src = picked[h][:].rearrange("p t (c i) -> p c t i", i=4)
+            if h == 0:
+                nc.scalar.copy(out=dst, in_=src)
+            else:
+                nc.vector.tensor_copy(out=dst, in_=src)
+            picked_bf.append(woven)
+
+        neg_scores = sb.tile([P, I], F32, name="neg_scores")
+        neg_max = [sb.tile([P, 1], F32, name="neg_max%d" % h) for h in range(2)]
+        banks = []
+        for h in range(2):
+            k_codes = sb.tile([P, HALF], U32, name="k_codes%d" % h, align_bytes=64)
+            k_sc = sb.tile([P, HALF], U8, name="k_sc%d" % h, align_bytes=64)
+            nc.vector.quantize_mx(out=k_codes[:].bitcast(FP8X4), scales=k_sc[:], in_=picked_bf[h][:])
+            bank = score_ps.tile([P, HALF], F32, name="score_bank")
+            nc.tensor.matmul_mx(
+                out=bank[:],
+                lhsT=q_codes[:].bitcast(FP8X4),
+                lhsT_scale=q_sc[:],
+                rhs=k_codes[:].bitcast(FP8X4),
+                rhs_scale=k_sc[:],
+                start=True,
+                stop=True,
+            )
+            banks.append(bank)
+        nc.vector.tensor_scalar(
+            out=neg_scores[:, 0:HALF], in0=banks[0][:], scalar1=-1.0, scalar2=None,
+            op0=ALU.mult, op1=ALU.min, accum_out=neg_max[0][:],
+        )
+        nc.vector.tensor_scalar(
+            out=neg_scores[:, HALF:I], in0=banks[1][:], scalar1=-1.0, scalar2=neg_max[0][:],
+            op0=ALU.mult, op1=ALU.min, accum_out=neg_max[1][:],
+        )
+
+        prob = sb.tile([P, I], F32, name="prob")
+        total = sb.tile([P, 1], F32, name="total")
+        nc.scalar.activation(prob[:], neg_scores[:], EXP, bias=neg_max[1][:], scale=-1.0, accum_out=total[:])
+        inv = sb.tile([P, 1], F32, name="inv")
+        nc.vector.reciprocal(inv[:], total[:])
+        for h in range(2):
+            cols = slice(h * HALF, (h + 1) * HALF)
+            res = sb.tile([P, HALF], F32, name="res%d" % h)
+            nc.vector.tensor_scalar(
+                out=res[:], in0=prob[:, cols], scalar1=inv[:], scalar2=float(I), op0=ALU.mult, op1=ALU.mult
+            )
+            nc.sync.dma_start(out=out[:, cols], in_=res[:])

@@ -29,6 +29,7 @@ def tile_attend_grouppick_fresh_kernel(tc, emb_words, emb_scales, wk, query, off
         score_ps = ctx.enter_context(tc.psum_pool(name="score_ps", bufs=2))
 
         offsets = sb.tile([P, I // 16], U16, name="offsets")
+        nc.sync.dma_start(offsets[:], offs)
 
         emb_sc = sb.tile([P, T], U8, name="emb_sc", align_bytes=64)
         nc.vector.memset(emb_sc[:].bitcast(I32), 0)
@@ -41,8 +42,8 @@ def tile_attend_grouppick_fresh_kernel(tc, emb_words, emb_scales, wk, query, off
         wk_rows = wk.rearrange("(p t) d -> p t d", t=PACK)
         wk_raw = []
         for c in range(2):
-            raw = sb.tile([P, PACK, D // 2], F32, name="wk_raw%d" % c)
-            nc.sync.dma_start(out=raw[:], in_=wk_rows[:, :, c * (D // 2) : (c + 1) * (D // 2)])
+            raw = sb.tile([P, 2, D], F32, name="wk_raw%d" % c, tag="raw%d" % c)
+            nc.sync.dma_start(out=raw[:], in_=wk_rows[:, 2 * c : 2 * c + 2, :])
             wk_raw.append(raw)
 
         emb_bytes = emb_words[0].rearrange("p n t -> p (n t)")
@@ -55,13 +56,6 @@ def tile_attend_grouppick_fresh_kernel(tc, emb_words, emb_scales, wk, query, off
             )
             emb_codes.append(codes)
 
-        nc.sync.dma_start(offsets[:], offs)
-
-        q_raw = sb.tile([P, PACK, Q], F32, name="q_raw")
-        q_planes = query.rearrange("(b j r) q -> j b r q", j=PACK, r=8)
-        for j in range(PACK):
-            nc.sync.dma_start(out=q_raw[:, j, :], in_=q_planes[j])
-
         warm_in = sb.tile([P, 1], F32, name="warm_in")
         warm_out = sb.tile([P, 1], F32, name="warm_out")
         nc.vector.memset(warm_in[:], 0.0)
@@ -69,13 +63,18 @@ def tile_attend_grouppick_fresh_kernel(tc, emb_words, emb_scales, wk, query, off
 
         wk_bf = [sb.tile([P, P * PACK], BF16, name="wk_bf%d" % j, align_bytes=64) for j in range(PACK)]
         for c in range(2):
-            src = wk_raw[c][:].rearrange("p t (b j h i) -> p j b h t i", j=PACK, h=2, i=4)
+            src = wk_raw[c][:].rearrange("p t (b j r) -> p j b r t", j=PACK, r=8)
             for j in range(PACK):
-                dst = wk_bf[j][:].rearrange("p (c b h i t) -> p c b h t i", c=2, h=2, i=4, t=PACK)
+                dst = wk_bf[j][:].rearrange("p (b r c t) -> p c b r t", c=2, r=8, t=2)
                 if j < 2:
                     nc.vector.tensor_copy(out=dst[:, c], in_=src[:, j])
                 else:
                     nc.scalar.copy(out=dst[:, c], in_=src[:, j])
+
+        q_raw = sb.tile([P, PACK, Q], F32, name="q_raw", tag="raw0")
+        q_planes = query.rearrange("(b j r) q -> j b r q", j=PACK, r=8)
+        for j in range(PACK):
+            nc.sync.dma_start(out=q_raw[:, j, :], in_=q_planes[j])
 
         keys = []
         for j in range(PACK):
@@ -83,7 +82,7 @@ def tile_attend_grouppick_fresh_kernel(tc, emb_words, emb_scales, wk, query, off
             wk_sc = sb.tile([P, P], U8, name="wk_sc%d" % j, align_bytes=64)
             nc.vector.quantize_mx(out=wk_codes[:].bitcast(FP8X4), scales=wk_sc[:], in_=wk_bf[j][:])
             key = sb.tile([P, T], F32, name="key%d" % j)
-            cuts = (0, BANK, BANK + BANK // 2, T) if j == 0 else (0, BANK, T)
+            cuts = range(0, T + 1, BANK // 2 if j == 0 else BANK)
             for a, b in zip(cuts, cuts[1:]):
                 h = a // BANK
                 bank = key_ps.tile([P, b - a], F32, name="key_bank")
@@ -96,7 +95,7 @@ def tile_attend_grouppick_fresh_kernel(tc, emb_words, emb_scales, wk, query, off
                     start=True,
                     stop=True,
                 )
-                if j == 0 and a == BANK:
+                if j == 0 and a % BANK == 0:
                     nc.vector.tensor_copy(out=key[:, a:b], in_=bank[:])
                 else:
                     nc.scalar.copy(out=key[:, a:b], in_=bank[:])
@@ -169,4 +168,5 @@ def tile_attend_grouppick_fresh_kernel(tc, emb_words, emb_scales, wk, query, off
             nc.vector.tensor_scalar(
                 out=res[:], in0=prob[:, cols], scalar1=inv[:], scalar2=float(I), op0=ALU.mult, op1=ALU.mult
             )
-            nc.sync.dma_start(out=out[:, cols], in_=res[:])
+            queue = nc.sync if h == 0 else nc.scalar
+            queue.dma_start(out=out[:, cols], in_=res[:])

@@ -14,6 +14,7 @@ U8 = mybir.dt.uint8
 FP8X4 = mybir.dt.float8_e4m3fn_x4
 ALU = mybir.AluOpType
 EXP = mybir.ActivationFunctionType.Exp
+COPY = mybir.ActivationFunctionType.Copy
 
 P = 128
 PACK = 4
@@ -56,17 +57,14 @@ def tile_attend_grouppick_fresh_kernel(tc, emb_words, emb_scales, wk, query, off
             )
             emb_codes.append(codes)
 
-        warm_in = sb.tile([P, 1], F32, name="warm_in")
-        warm_out = sb.tile([P, 1], F32, name="warm_out")
-        nc.vector.memset(warm_in[:], 0.0)
-        nc.scalar.activation(warm_out[:], warm_in[:], EXP)
-
         wk_bf = [sb.tile([P, P * PACK], BF16, name="wk_bf%d" % j, align_bytes=64) for j in range(PACK)]
         for c in range(2):
             src = wk_raw[c][:].rearrange("p t (b j r) -> p j b r t", j=PACK, r=8)
             for j in range(PACK):
                 dst = wk_bf[j][:].rearrange("p (b r c t) -> p c b r t", c=2, r=8, t=2)
-                if j < 2:
+                if j >= 2 and c == 0:
+                    nc.scalar.activation(dst[:, c], src[:, j], COPY)
+                elif j < 2:
                     nc.vector.tensor_copy(out=dst[:, c], in_=src[:, j])
                 else:
                     nc.scalar.copy(out=dst[:, c], in_=src[:, j])
@@ -82,7 +80,7 @@ def tile_attend_grouppick_fresh_kernel(tc, emb_words, emb_scales, wk, query, off
             wk_sc = sb.tile([P, P], U8, name="wk_sc%d" % j, align_bytes=64)
             nc.vector.quantize_mx(out=wk_codes[:].bitcast(FP8X4), scales=wk_sc[:], in_=wk_bf[j][:])
             key = sb.tile([P, T], F32, name="key%d" % j)
-            cuts = range(0, T + 1, BANK // 2 if j == 0 else BANK)
+            cuts = range(0, T + 1, BANK // 2 if j < 2 else BANK)
             for a, b in zip(cuts, cuts[1:]):
                 h = a // BANK
                 bank = key_ps.tile([P, b - a], F32, name="key_bank")
@@ -107,13 +105,14 @@ def tile_attend_grouppick_fresh_kernel(tc, emb_words, emb_scales, wk, query, off
             in_=q_raw[:].rearrange("p t (c i) -> p c t i", i=4),
         )
 
-        picked = [sb.tile([P, PACK, HALF], BF16, name="picked%d" % h) for h in range(2)]
-        for j in range(PACK):
-            for h in range(2):
-                nc.vector.tensor_copy(
-                    out=picked[h][:, j, :],
-                    in_=keys[j][:].indirect(offsets[:, h * (HALF // 16) : (h + 1) * (HALF // 16)]),
-                )
+        picked = sb.tile([P, PACK, I], BF16, name="picked")
+        for j in range(PACK - 1):
+            nc.vector.tensor_copy(out=picked[:, j, :], in_=keys[j][:].indirect(offsets[:]))
+        for h in range(2):
+            nc.vector.tensor_copy(
+                out=picked[:, PACK - 1, h * HALF : (h + 1) * HALF],
+                in_=keys[PACK - 1][:].indirect(offsets[:, h * (HALF // 16) : (h + 1) * (HALF // 16)]),
+            )
 
         q_codes = sb.tile([P, Q], U32, name="q_codes", align_bytes=64)
         q_sc = sb.tile([P, Q], U8, name="q_sc", align_bytes=64)
@@ -123,7 +122,7 @@ def tile_attend_grouppick_fresh_kernel(tc, emb_words, emb_scales, wk, query, off
         for h in range(2):
             woven = sb.tile([P, HALF * PACK], BF16, name="woven%d" % h, align_bytes=64)
             dst = woven[:].rearrange("p (c i t) -> p c t i", i=4, t=PACK)
-            src = picked[h][:].rearrange("p t (c i) -> p c t i", i=4)
+            src = picked[:, :, h * HALF : (h + 1) * HALF].rearrange("p t (c i) -> p c t i", i=4)
             if h == 0:
                 nc.scalar.copy(out=dst, in_=src)
             else:

@@ -20,6 +20,7 @@ P = 128
 PACK = 4
 BANK = 512
 HALF = I // 2
+PIECE = T // 4
 
 
 def tile_attend_grouppick_fresh_kernel(tc, emb_words, emb_scales, wk, query, offs, out):
@@ -32,12 +33,12 @@ def tile_attend_grouppick_fresh_kernel(tc, emb_words, emb_scales, wk, query, off
         offsets = sb.tile([P, I // 16], U16, name="offsets")
         nc.sync.dma_start(offsets[:], offs)
 
-        emb_sc = sb.tile([P, T], U8, name="emb_sc", align_bytes=64)
+        emb_sc = sb.tile([P, PIECE], U8, name="emb_sc", align_bytes=64)
         nc.vector.memset(emb_sc[:].bitcast(I32), 0)
         for g in range(4):
             nc.scalar.dma_start(
-                out=emb_sc[32 * g : 32 * g + 4, :].bitcast(I32),
-                in_=emb_scales[0, 4 * g : 4 * g + 4, :].bitcast(I32),
+                out=emb_sc[32 * g : 32 * g + 16, :].bitcast(I32),
+                in_=emb_scales[0, 4 * g : 4 * g + 4, :].bitcast(I32).rearrange("r (c n) -> c r n", c=4),
             )
 
         wk_rows = wk.rearrange("(p t) d -> p t d", t=PACK)
@@ -80,23 +81,23 @@ def tile_attend_grouppick_fresh_kernel(tc, emb_words, emb_scales, wk, query, off
             wk_sc = sb.tile([P, P], U8, name="wk_sc%d" % j, align_bytes=64)
             nc.vector.quantize_mx(out=wk_codes[:].bitcast(FP8X4), scales=wk_sc[:], in_=wk_bf[j][:])
             key = sb.tile([P, T], F32, name="key%d" % j)
-            cuts = range(0, T + 1, BANK // 2 if j < 2 else BANK)
-            for a, b in zip(cuts, cuts[1:]):
-                h = a // BANK
-                bank = key_ps.tile([P, b - a], F32, name="key_bank")
-                nc.tensor.matmul_mx(
-                    out=bank[:],
-                    lhsT=wk_codes[:].bitcast(FP8X4),
-                    lhsT_scale=wk_sc[:],
-                    rhs=emb_codes[h][:, a - h * BANK : b - h * BANK].bitcast(FP8X4),
-                    rhs_scale=emb_sc[:, a:b],
-                    start=True,
-                    stop=True,
-                )
+            width = PIECE if j < 2 else BANK
+            for a in range(0, T, width):
+                bank = key_ps.tile([P, width], F32, name="key_bank")
+                for c in range(a // PIECE, (a + width) // PIECE):
+                    nc.tensor.matmul_mx(
+                        out=bank[:, c * PIECE - a : (c + 1) * PIECE - a],
+                        lhsT=wk_codes[:].bitcast(FP8X4),
+                        lhsT_scale=wk_sc[:],
+                        rhs=emb_codes[c // 2][:, c % 2 * PIECE : (c % 2 + 1) * PIECE].bitcast(FP8X4),
+                        rhs_scale=emb_sc[4 * c :, :],
+                        start=True,
+                        stop=True,
+                    )
                 if j == 0 and a % BANK == 0:
-                    nc.vector.tensor_copy(out=key[:, a:b], in_=bank[:])
+                    nc.vector.tensor_copy(out=key[:, a : a + width], in_=bank[:])
                 else:
-                    nc.scalar.copy(out=key[:, a:b], in_=bank[:])
+                    nc.scalar.copy(out=key[:, a : a + width], in_=bank[:])
             keys.append(key)
 
         q_bf = sb.tile([P, Q * PACK], BF16, name="q_bf", tag="stationary%d" % (PACK - 1), align_bytes=64)

@@ -106,7 +106,7 @@ def tile_attend_grouppick_fresh_kernel(tc, emb_words, emb_scales, wk, query, off
             in_=q_raw[:].rearrange("p t (c i) -> p c t i", i=4),
         )
 
-        picked = sb.tile([P, PACK, I], BF16, name="picked")
+        picked = sb.tile([P, PACK, I], F32, name="picked")
         for j in range(PACK - 1):
             nc.vector.tensor_copy(out=picked[:, j, :], in_=keys[j][:].indirect(offsets[:]))
         for h in range(2):
@@ -115,28 +115,30 @@ def tile_attend_grouppick_fresh_kernel(tc, emb_words, emb_scales, wk, query, off
                 in_=keys[PACK - 1][:].indirect(offsets[:, h * (HALF // 16) : (h + 1) * (HALF // 16)]),
             )
 
+        woven = [sb.tile([P, HALF * PACK], BF16, name="woven%d" % h, tag="woven%d" % h, align_bytes=64) for h in range(2)]
+
+        def weave(copy, a, b):
+            first = a // HALF * HALF
+            dst = woven[a // HALF][:, (a - first) * PACK : (b - first) * PACK]
+            copy(
+                out=dst.rearrange("p (c i t) -> p c t i", i=4, t=PACK),
+                in_=picked[:, :, a:b].rearrange("p t (c i) -> p c t i", i=4),
+            )
+
+        weave(nc.scalar.copy, 0, HALF // 2)
+        weave(nc.vector.tensor_copy, HALF // 2, HALF)
         q_codes = sb.tile([P, Q], U32, name="q_codes", align_bytes=64)
         q_sc = sb.tile([P, Q], U8, name="q_sc", align_bytes=64)
         nc.vector.quantize_mx(out=q_codes[:].bitcast(FP8X4), scales=q_sc[:], in_=q_bf[:])
+        weave(nc.vector.tensor_copy, HALF, I - HALF // 4)
+        weave(nc.scalar.copy, I - HALF // 4, I)
 
-        picked_bf = []
-        for h in range(2):
-            woven = sb.tile([P, HALF * PACK], BF16, name="woven%d" % h, align_bytes=64)
-            dst = woven[:].rearrange("p (c i t) -> p c t i", i=4, t=PACK)
-            src = picked[:, :, h * HALF : (h + 1) * HALF].rearrange("p t (c i) -> p c t i", i=4)
-            if h == 0:
-                nc.scalar.copy(out=dst, in_=src)
-            else:
-                nc.vector.tensor_copy(out=dst, in_=src)
-            picked_bf.append(woven)
-
-        neg_scores = sb.tile([P, I], F32, name="neg_scores")
         neg_max = [sb.tile([P, 1], F32, name="neg_max%d" % h) for h in range(2)]
         banks = []
         for h in range(2):
             k_codes = sb.tile([P, HALF], U32, name="k_codes%d" % h, align_bytes=64)
             k_sc = sb.tile([P, HALF], U8, name="k_sc%d" % h, align_bytes=64)
-            nc.vector.quantize_mx(out=k_codes[:].bitcast(FP8X4), scales=k_sc[:], in_=picked_bf[h][:])
+            nc.vector.quantize_mx(out=k_codes[:].bitcast(FP8X4), scales=k_sc[:], in_=woven[h][:])
             bank = score_ps.tile([P, HALF], F32, name="score_bank")
             nc.tensor.matmul_mx(
                 out=bank[:],
@@ -148,6 +150,7 @@ def tile_attend_grouppick_fresh_kernel(tc, emb_words, emb_scales, wk, query, off
                 stop=True,
             )
             banks.append(bank)
+        neg_scores = sb.tile([P, I], F32, name="neg_scores", tag="woven1", align_bytes=64)
         nc.vector.tensor_scalar(
             out=neg_scores[:, 0:HALF], in0=banks[0][:], scalar1=-1.0, scalar2=None,
             op0=ALU.mult, op1=ALU.min, accum_out=neg_max[0][:],

@@ -27,19 +27,13 @@ def tile_attend_grouppick_fresh_kernel(tc, emb_words, emb_scales, wk, query, off
     nc = tc.nc
     with ExitStack() as ctx:
         sb = ctx.enter_context(tc.tile_pool(name="sb", bufs=1))
-        key_ps = ctx.enter_context(tc.psum_pool(name="key_ps", bufs=6))
-        score_ps = ctx.enter_context(tc.psum_pool(name="score_ps", bufs=2))
+        key_ps = ctx.enter_context(tc.psum_pool(name="key_ps", bufs=7))
+        score_ps = ctx.enter_context(tc.psum_pool(name="score_ps", bufs=1))
 
         offsets = sb.tile([P, I // 16], U16, name="offsets")
-        nc.sync.dma_start(offsets[:], offs)
 
         emb_sc = sb.tile([P, PIECE], U8, name="emb_sc", align_bytes=64)
         nc.vector.memset(emb_sc[:].bitcast(I32), 0)
-        for g in range(4):
-            nc.scalar.dma_start(
-                out=emb_sc[32 * g : 32 * g + 16, :].bitcast(I32),
-                in_=emb_scales[0, 4 * g : 4 * g + 4, :].bitcast(I32).rearrange("r (c n) -> c r n", c=4),
-            )
 
         wk_rows = wk.rearrange("(p t) d -> p t d", t=PACK)
         wk_raw = []
@@ -47,6 +41,12 @@ def tile_attend_grouppick_fresh_kernel(tc, emb_words, emb_scales, wk, query, off
             raw = sb.tile([P, 2, D], F32, name="wk_raw%d" % c, tag="raw%d" % c)
             nc.sync.dma_start(out=raw[:], in_=wk_rows[:, 2 * c : 2 * c + 2, :])
             wk_raw.append(raw)
+
+        for g in range(4):
+            nc.sync.dma_start(
+                out=emb_sc[32 * g : 32 * g + 16, :].bitcast(I32),
+                in_=emb_scales[0, 4 * g : 4 * g + 4, :].bitcast(I32).rearrange("r (c n) -> c r n", c=4),
+            )
 
         emb_bytes = emb_words[0].rearrange("p n t -> p (n t)")
         emb_codes = []
@@ -58,22 +58,23 @@ def tile_attend_grouppick_fresh_kernel(tc, emb_words, emb_scales, wk, query, off
             )
             emb_codes.append(codes)
 
+        nc.sync.dma_start(offsets[:], offs)
+        q_raw = sb.tile([P, PACK * Q], F32, name="q_raw")
+        q_pairs = query.rearrange("(b h r e) q -> h b r (e q)", h=2, r=8, e=2)
+        for h in range(2):
+            nc.sync.dma_start(out=q_raw[:, h * 2 * Q : (h + 1) * 2 * Q], in_=q_pairs[h])
+
         wk_bf = [sb.tile([P, P * PACK], BF16, name="wk_bf%d" % j, align_bytes=64) for j in range(PACK)]
         for c in range(2):
-            src = wk_raw[c][:].rearrange("p t (b j r) -> p j b r t", j=PACK, r=8)
+            src = wk_raw[c][:].rearrange("p t (b h r e) -> p h e b r t", h=2, r=8, e=2)
             for j in range(PACK):
                 dst = wk_bf[j][:].rearrange("p (b r c t) -> p c b r t", c=2, r=8, t=2)
                 if j >= 2 and c == 0:
-                    nc.scalar.activation(dst[:, c], src[:, j], COPY)
+                    nc.scalar.activation(dst[:, c], src[:, j // 2, j % 2], COPY)
                 elif j < 2:
-                    nc.vector.tensor_copy(out=dst[:, c], in_=src[:, j])
+                    nc.vector.tensor_copy(out=dst[:, c], in_=src[:, j // 2, j % 2])
                 else:
-                    nc.scalar.copy(out=dst[:, c], in_=src[:, j])
-
-        q_raw = sb.tile([P, PACK, Q], F32, name="q_raw", tag="raw0")
-        q_planes = query.rearrange("(b j r) q -> j b r q", j=PACK, r=8)
-        for j in range(PACK):
-            nc.sync.dma_start(out=q_raw[:, j, :], in_=q_planes[j])
+                    nc.scalar.copy(out=dst[:, c], in_=src[:, j // 2, j % 2])
 
         keys = []
         for j in range(PACK):
@@ -94,7 +95,7 @@ def tile_attend_grouppick_fresh_kernel(tc, emb_words, emb_scales, wk, query, off
                         start=True,
                         stop=True,
                     )
-                if j == 0 and a % BANK == 0:
+                if j == 0 and a in (0, T - PIECE):
                     nc.vector.tensor_copy(out=key[:, a : a + width], in_=bank[:])
                 else:
                     nc.scalar.copy(out=key[:, a : a + width], in_=bank[:])
@@ -103,8 +104,11 @@ def tile_attend_grouppick_fresh_kernel(tc, emb_words, emb_scales, wk, query, off
         q_bf = sb.tile([P, Q * PACK], BF16, name="q_bf", tag="stationary%d" % (PACK - 1), align_bytes=64)
         nc.scalar.copy(
             out=q_bf[:].rearrange("p (c i t) -> p c t i", i=4, t=PACK),
-            in_=q_raw[:].rearrange("p t (c i) -> p c t i", i=4),
+            in_=q_raw[:].rearrange("p (t c i) -> p c t i", i=4, t=PACK),
         )
+        q_codes = sb.tile([P, Q], U32, name="q_codes", align_bytes=64)
+        q_sc = sb.tile([P, Q], U8, name="q_sc", align_bytes=64)
+        nc.vector.quantize_mx(out=q_codes[:].bitcast(FP8X4), scales=q_sc[:], in_=q_bf[:])
 
         picked = sb.tile([P, PACK, I], F32, name="picked")
         for j in range(PACK - 1):
@@ -115,33 +119,29 @@ def tile_attend_grouppick_fresh_kernel(tc, emb_words, emb_scales, wk, query, off
                 in_=keys[PACK - 1][:].indirect(offsets[:, h * (HALF // 16) : (h + 1) * (HALF // 16)]),
             )
 
-        woven = [sb.tile([P, HALF * PACK], BF16, name="woven%d" % h, tag="woven%d" % h, align_bytes=64) for h in range(2)]
+        QUARTER = I // 4
+        woven = [
+            sb.tile([P, QUARTER * PACK], BF16, name="woven%d" % u, tag="woven%d" % u, align_bytes=64) for u in range(4)
+        ]
 
-        def weave(copy, a, b):
-            first = a // HALF * HALF
-            dst = woven[a // HALF][:, (a - first) * PACK : (b - first) * PACK]
+        def weave(copy, u):
             copy(
-                out=dst.rearrange("p (c i t) -> p c t i", i=4, t=PACK),
-                in_=picked[:, :, a:b].rearrange("p t (c i) -> p c t i", i=4),
+                out=woven[u][:].rearrange("p (c i t) -> p c t i", i=4, t=PACK),
+                in_=picked[:, :, u * QUARTER : (u + 1) * QUARTER].rearrange("p t (c i) -> p c t i", i=4),
             )
 
-        weave(nc.scalar.copy, 0, HALF // 2)
-        weave(nc.vector.tensor_copy, HALF // 2, HALF)
-        q_codes = sb.tile([P, Q], U32, name="q_codes", align_bytes=64)
-        q_sc = sb.tile([P, Q], U8, name="q_sc", align_bytes=64)
-        nc.vector.quantize_mx(out=q_codes[:].bitcast(FP8X4), scales=q_sc[:], in_=q_bf[:])
-        weave(nc.vector.tensor_copy, HALF, I - HALF // 4)
-        weave(nc.scalar.copy, I - HALF // 4, I)
+        weave(nc.scalar.copy, 0)
+        weave(nc.vector.tensor_copy, 1)
+        weave(nc.vector.tensor_copy, 2)
+        weave(nc.scalar.copy, 3)
 
-        neg_max = [sb.tile([P, 1], F32, name="neg_max%d" % h) for h in range(2)]
-        banks = []
-        for h in range(2):
-            k_codes = sb.tile([P, HALF], U32, name="k_codes%d" % h, align_bytes=64)
-            k_sc = sb.tile([P, HALF], U8, name="k_sc%d" % h, align_bytes=64)
-            nc.vector.quantize_mx(out=k_codes[:].bitcast(FP8X4), scales=k_sc[:], in_=woven[h][:])
-            bank = score_ps.tile([P, HALF], F32, name="score_bank")
+        scores = score_ps.tile([P, I], F32, name="scores")
+        for u in (1, 2, 0, 3):
+            k_codes = sb.tile([P, QUARTER], U32, name="k_codes%d" % u, align_bytes=64)
+            k_sc = sb.tile([P, QUARTER], U8, name="k_sc%d" % u, align_bytes=64)
+            nc.vector.quantize_mx(out=k_codes[:].bitcast(FP8X4), scales=k_sc[:], in_=woven[u][:])
             nc.tensor.matmul_mx(
-                out=bank[:],
+                out=scores[:, u * QUARTER : (u + 1) * QUARTER],
                 lhsT=q_codes[:].bitcast(FP8X4),
                 lhsT_scale=q_sc[:],
                 rhs=k_codes[:].bitcast(FP8X4),
@@ -149,20 +149,12 @@ def tile_attend_grouppick_fresh_kernel(tc, emb_words, emb_scales, wk, query, off
                 start=True,
                 stop=True,
             )
-            banks.append(bank)
-        neg_scores = sb.tile([P, I], F32, name="neg_scores", tag="woven1", align_bytes=64)
-        nc.vector.tensor_scalar(
-            out=neg_scores[:, 0:HALF], in0=banks[0][:], scalar1=-1.0, scalar2=None,
-            op0=ALU.mult, op1=ALU.min, accum_out=neg_max[0][:],
-        )
-        nc.vector.tensor_scalar(
-            out=neg_scores[:, HALF:I], in0=banks[1][:], scalar1=-1.0, scalar2=neg_max[0][:],
-            op0=ALU.mult, op1=ALU.min, accum_out=neg_max[1][:],
-        )
+        neg_max = sb.tile([P, 1], F32, name="neg_max")
+        nc.vector.tensor_reduce(out=neg_max[:], in_=scores[:], axis=mybir.AxisListType.X, op=ALU.max, negate=True)
 
         prob = sb.tile([P, I], F32, name="prob")
         total = sb.tile([P, 1], F32, name="total")
-        nc.scalar.activation(prob[:], neg_scores[:], EXP, bias=neg_max[1][:], scale=-1.0, accum_out=total[:])
+        nc.scalar.activation(prob[:], scores[:], EXP, bias=neg_max[:], scale=1.0, accum_out=total[:])
         inv = sb.tile([P, 1], F32, name="inv")
         nc.vector.reciprocal(inv[:], total[:])
         for h in range(2):

@@ -51,7 +51,7 @@ def tile_attend_grouppick_fresh_kernel(tc, emb_words, emb_scales, wk, query, off
         emb_bytes = emb_words[0].rearrange("p n t -> p (n t)")
         emb_codes = []
         for h in range(2):
-            codes = sb.tile([P, BANK], U32, name="emb_codes%d" % h, align_bytes=64)
+            codes = sb.tile([P, BANK], U32, name="emb_codes%d" % h, tag="moving%d" % (h + 1), align_bytes=64)
             nc.sync.dma_start(
                 out=codes[:].bitcast(I32),
                 in_=emb_bytes[:, h * BANK * PACK : (h + 1) * BANK * PACK].bitcast(I32),
@@ -82,23 +82,29 @@ def tile_attend_grouppick_fresh_kernel(tc, emb_words, emb_scales, wk, query, off
             wk_sc = sb.tile([P, P], U8, name="wk_sc%d" % j, align_bytes=64)
             nc.vector.quantize_mx(out=wk_codes[:].bitcast(FP8X4), scales=wk_sc[:], in_=wk_bf[j][:])
             key = sb.tile([P, T], F32, name="key%d" % j)
-            width = PIECE if j < 2 else BANK
-            for a in range(0, T, width):
-                bank = key_ps.tile([P, width], F32, name="key_bank")
-                for c in range(a // PIECE, (a + width) // PIECE):
+            if j == 0:
+                cuts = [0, PIECE, 2 * PIECE, 3 * PIECE, 3 * PIECE + P, T]
+            elif j == 2:
+                cuts = [0, PIECE, BANK, T]
+            else:
+                cuts = list(range(0, T + 1, PIECE if j == 1 else BANK))
+            for first, last in zip(cuts, cuts[1:]):
+                bank = key_ps.tile([P, last - first], F32, name="key_bank")
+                for a in range(first, last, PIECE):
+                    b = min(a + PIECE, last)
                     nc.tensor.matmul_mx(
-                        out=bank[:, c * PIECE - a : (c + 1) * PIECE - a],
+                        out=bank[:, a - first : b - first],
                         lhsT=wk_codes[:].bitcast(FP8X4),
                         lhsT_scale=wk_sc[:],
-                        rhs=emb_codes[c // 2][:, c % 2 * PIECE : (c % 2 + 1) * PIECE].bitcast(FP8X4),
-                        rhs_scale=emb_sc[4 * c :, :],
+                        rhs=emb_codes[a // BANK][:, a % BANK : a % BANK + b - a].bitcast(FP8X4),
+                        rhs_scale=emb_sc[4 * (a // PIECE) :, a % PIECE : a % PIECE + b - a],
                         start=True,
                         stop=True,
                     )
-                if j == 0 and a in (0, T - PIECE):
-                    nc.vector.tensor_copy(out=key[:, a : a + width], in_=bank[:])
+                if j == 0 and (first == 0 or first >= 3 * PIECE):
+                    nc.vector.tensor_copy(out=key[:, first:last], in_=bank[:])
                 else:
-                    nc.scalar.copy(out=key[:, a : a + width], in_=bank[:])
+                    nc.scalar.copy(out=key[:, first:last], in_=bank[:])
             keys.append(key)
 
         q_bf = sb.tile([P, Q * PACK], BF16, name="q_bf", tag="stationary%d" % (PACK - 1), align_bytes=64)
@@ -121,7 +127,7 @@ def tile_attend_grouppick_fresh_kernel(tc, emb_words, emb_scales, wk, query, off
 
         QUARTER = I // 4
         woven = [
-            sb.tile([P, QUARTER * PACK], BF16, name="woven%d" % u, tag="woven%d" % u, align_bytes=64) for u in range(4)
+            sb.tile([P, QUARTER * PACK], BF16, name="woven%d" % u, tag="moving%d" % u, align_bytes=64) for u in range(4)
         ]
 
         def weave(copy, u):
@@ -130,9 +136,17 @@ def tile_attend_grouppick_fresh_kernel(tc, emb_words, emb_scales, wk, query, off
                 in_=picked[:, :, u * QUARTER : (u + 1) * QUARTER].rearrange("p t (c i) -> p c t i", i=4),
             )
 
+        def weave_pair(copy, u, c):
+            copy(
+                out=woven[u][:].rearrange("p (i c t) -> p c i t", c=2, t=2)[:, c],
+                in_=picked[:, 2 * c : 2 * c + 2, u * QUARTER : (u + 1) * QUARTER].rearrange("p t i -> p i t"),
+            )
+
+        weave_pair(nc.scalar.copy, 1, 0)
+        weave_pair(nc.scalar.copy, 2, 0)
         weave(nc.scalar.copy, 0)
-        weave(nc.vector.tensor_copy, 1)
-        weave(nc.vector.tensor_copy, 2)
+        weave_pair(nc.vector.tensor_copy, 1, 1)
+        weave_pair(nc.vector.tensor_copy, 2, 1)
         weave(nc.scalar.copy, 3)
 
         scores = score_ps.tile([P, I], F32, name="scores")

@@ -86,8 +86,10 @@ def tile_attend_grouppick_fresh_kernel(tc, emb_words, emb_scales, wk, query, off
                 cuts = [0, PIECE, 2 * PIECE, 3 * PIECE, 3 * PIECE + P, T]
             elif j == 2:
                 cuts = [0, PIECE, BANK, T]
+            elif j == 3:
+                cuts = [0, BANK, BANK + PIECE, T]
             else:
-                cuts = list(range(0, T + 1, PIECE if j == 1 else BANK))
+                cuts = list(range(0, T + 1, PIECE))
             for first, last in zip(cuts, cuts[1:]):
                 bank = key_ps.tile([P, last - first], F32, name="key_bank")
                 for a in range(first, last, PIECE):
@@ -126,24 +128,26 @@ def tile_attend_grouppick_fresh_kernel(tc, emb_words, emb_scales, wk, query, off
             )
 
         QUARTER = I // 4
-        woven = [
-            sb.tile([P, QUARTER * PACK], BF16, name="woven%d" % u, tag="moving%d" % u, align_bytes=64) for u in range(4)
-        ]
+        outer = [sb.tile([P, QUARTER * PACK], BF16, name="outer%d" % e, align_bytes=64) for e in range(2)]
+        middle = sb.tile([P, HALF * PACK], BF16, name="middle", tag="moving2", align_bytes=64)
+        woven = [outer[0][:], middle[:, 0 : QUARTER * PACK], middle[:, QUARTER * PACK : HALF * PACK], outer[1][:]]
 
         def weave(copy, u):
             copy(
-                out=woven[u][:].rearrange("p (c i t) -> p c t i", i=4, t=PACK),
+                out=woven[u].rearrange("p (c i t) -> p c t i", i=4, t=PACK),
                 in_=picked[:, :, u * QUARTER : (u + 1) * QUARTER].rearrange("p t (c i) -> p c t i", i=4),
             )
 
         def weave_pair(copy, u, c):
             copy(
-                out=woven[u][:].rearrange("p (i c t) -> p c i t", c=2, t=2)[:, c],
+                out=woven[u].rearrange("p (i c t) -> p c i t", c=2, t=2)[:, c],
                 in_=picked[:, 2 * c : 2 * c + 2, u * QUARTER : (u + 1) * QUARTER].rearrange("p t i -> p i t"),
             )
 
-        weave_pair(nc.scalar.copy, 1, 0)
-        weave_pair(nc.scalar.copy, 2, 0)
+        nc.scalar.copy(
+            out=middle[:].rearrange("p (i c t) -> p c i t", c=2, t=2)[:, 0],
+            in_=picked[:, 0:2, QUARTER : I - QUARTER].rearrange("p t i -> p i t"),
+        )
         weave(nc.scalar.copy, 0)
         weave_pair(nc.vector.tensor_copy, 1, 1)
         weave_pair(nc.vector.tensor_copy, 2, 1)
@@ -153,7 +157,7 @@ def tile_attend_grouppick_fresh_kernel(tc, emb_words, emb_scales, wk, query, off
         for u in (1, 2, 0, 3):
             k_codes = sb.tile([P, QUARTER], U32, name="k_codes%d" % u, align_bytes=64)
             k_sc = sb.tile([P, QUARTER], U8, name="k_sc%d" % u, align_bytes=64)
-            nc.vector.quantize_mx(out=k_codes[:].bitcast(FP8X4), scales=k_sc[:], in_=woven[u][:])
+            nc.vector.quantize_mx(out=k_codes[:].bitcast(FP8X4), scales=k_sc[:], in_=woven[u])
             nc.tensor.matmul_mx(
                 out=scores[:, u * QUARTER : (u + 1) * QUARTER],
                 lhsT=q_codes[:].bitcast(FP8X4),

@@ -18,9 +18,20 @@ COPY = mybir.ActivationFunctionType.Copy
 
 P = 128
 PACK = 4
-BANK = 512
-HALF = I // 2
-PIECE = T // 4
+LIST_ROWS = 16
+T_HALF = T // 2
+T_QUARTER = T // 4
+I_HALF = I // 2
+I_QUARTER = I // 4
+
+QUARTER_CUTS = list(range(0, T + 1, T_QUARTER))
+PLANE_CUTS = [
+    QUARTER_CUTS[:-1] + [T - P, T],
+    QUARTER_CUTS,
+    QUARTER_CUTS,
+    [0] + QUARTER_CUTS[2:],
+]
+VECTOR_COPIES = (0, 2 * T_QUARTER)
 
 
 def tile_attend_grouppick_fresh_kernel(tc, emb_words, emb_scales, wk, query, offs, out):
@@ -30,16 +41,16 @@ def tile_attend_grouppick_fresh_kernel(tc, emb_words, emb_scales, wk, query, off
         key_ps = ctx.enter_context(tc.psum_pool(name="key_ps", bufs=7))
         score_ps = ctx.enter_context(tc.psum_pool(name="score_ps", bufs=1))
 
-        offsets = sb.tile([P, I // 16], U16, name="offsets")
+        offsets = sb.tile([P, I // LIST_ROWS], U16, name="offsets")
 
-        emb_sc = sb.tile([P, PIECE], U8, name="emb_sc", align_bytes=64)
+        emb_sc = sb.tile([P, T_QUARTER], U8, name="emb_sc", align_bytes=64)
         nc.vector.memset(emb_sc[:].bitcast(I32), 0)
 
         wk_rows = wk.rearrange("(p t) d -> p t d", t=PACK)
         wk_raw = []
-        for c in range(2):
-            raw = sb.tile([P, 2, D], F32, name="wk_raw%d" % c, tag="raw%d" % c)
-            nc.sync.dma_start(out=raw[:], in_=wk_rows[:, 2 * c : 2 * c + 2, :])
+        for pair in range(2):
+            raw = sb.tile([P, 2, D], F32, name="wk_raw%d" % pair)
+            nc.sync.dma_start(out=raw[:], in_=wk_rows[:, 2 * pair : 2 * pair + 2, :])
             wk_raw.append(raw)
 
         for g in range(4):
@@ -50,31 +61,32 @@ def tile_attend_grouppick_fresh_kernel(tc, emb_words, emb_scales, wk, query, off
 
         emb_bytes = emb_words[0].rearrange("p n t -> p (n t)")
         emb_codes = []
-        for h in range(2):
-            codes = sb.tile([P, BANK], U32, name="emb_codes%d" % h, tag="moving%d" % (h + 1), align_bytes=64)
+        for half in range(2):
+            codes = sb.tile([P, T_HALF], U32, name="emb_codes%d" % half, tag="emb%d" % half, align_bytes=64)
             nc.sync.dma_start(
                 out=codes[:].bitcast(I32),
-                in_=emb_bytes[:, h * BANK * PACK : (h + 1) * BANK * PACK].bitcast(I32),
+                in_=emb_bytes[:, half * T_HALF * PACK : (half + 1) * T_HALF * PACK].bitcast(I32),
             )
             emb_codes.append(codes)
 
         nc.sync.dma_start(offsets[:], offs)
+
         q_raw = sb.tile([P, PACK * Q], F32, name="q_raw")
-        q_pairs = query.rearrange("(b h r e) q -> h b r (e q)", h=2, r=8, e=2)
-        for h in range(2):
-            nc.sync.dma_start(out=q_raw[:, h * 2 * Q : (h + 1) * 2 * Q], in_=q_pairs[h])
+        q_planes = query.rearrange("(b j r) q -> j b r q", j=PACK, r=8)
+        for j in range(PACK):
+            nc.sync.dma_start(out=q_raw[:, j * Q : (j + 1) * Q], in_=q_planes[j])
 
         wk_bf = [sb.tile([P, P * PACK], BF16, name="wk_bf%d" % j, align_bytes=64) for j in range(PACK)]
-        for c in range(2):
-            src = wk_raw[c][:].rearrange("p t (b h r e) -> p h e b r t", h=2, r=8, e=2)
+        for pair in range(2):
+            src = wk_raw[pair][:].rearrange("p t (b j r) -> p j b r t", j=PACK, r=8)
             for j in range(PACK):
                 dst = wk_bf[j][:].rearrange("p (b r c t) -> p c b r t", c=2, r=8, t=2)
-                if j >= 2 and c == 0:
-                    nc.scalar.activation(dst[:, c], src[:, j // 2, j % 2], COPY)
-                elif j < 2:
-                    nc.vector.tensor_copy(out=dst[:, c], in_=src[:, j // 2, j % 2])
+                if j < 2:
+                    nc.vector.tensor_copy(out=dst[:, pair], in_=src[:, j])
+                elif pair == 0:
+                    nc.scalar.activation(dst[:, pair], src[:, j], COPY)
                 else:
-                    nc.scalar.copy(out=dst[:, c], in_=src[:, j // 2, j % 2])
+                    nc.scalar.copy(out=dst[:, pair], in_=src[:, j])
 
         keys = []
         for j in range(PACK):
@@ -82,28 +94,20 @@ def tile_attend_grouppick_fresh_kernel(tc, emb_words, emb_scales, wk, query, off
             wk_sc = sb.tile([P, P], U8, name="wk_sc%d" % j, align_bytes=64)
             nc.vector.quantize_mx(out=wk_codes[:].bitcast(FP8X4), scales=wk_sc[:], in_=wk_bf[j][:])
             key = sb.tile([P, T], F32, name="key%d" % j)
-            if j == 0:
-                cuts = [0, PIECE, 2 * PIECE, 3 * PIECE, 3 * PIECE + P, T]
-            elif j == 2:
-                cuts = [0, PIECE, BANK, T]
-            elif j == 3:
-                cuts = [0, BANK, BANK + PIECE, T]
-            else:
-                cuts = list(range(0, T + 1, PIECE))
-            for first, last in zip(cuts, cuts[1:]):
+            for first, last in zip(PLANE_CUTS[j], PLANE_CUTS[j][1:]):
                 bank = key_ps.tile([P, last - first], F32, name="key_bank")
-                for a in range(first, last, PIECE):
-                    b = min(a + PIECE, last)
+                for a in range(first, last, T_QUARTER):
+                    width = min(T_QUARTER, last - a)
                     nc.tensor.matmul_mx(
-                        out=bank[:, a - first : b - first],
+                        out=bank[:, a - first : a - first + width],
                         lhsT=wk_codes[:].bitcast(FP8X4),
                         lhsT_scale=wk_sc[:],
-                        rhs=emb_codes[a // BANK][:, a % BANK : a % BANK + b - a].bitcast(FP8X4),
-                        rhs_scale=emb_sc[4 * (a // PIECE) :, a % PIECE : a % PIECE + b - a],
+                        rhs=emb_codes[a // T_HALF][:, a % T_HALF : a % T_HALF + width].bitcast(FP8X4),
+                        rhs_scale=emb_sc[4 * (a // T_QUARTER) :, a % T_QUARTER : a % T_QUARTER + width],
                         start=True,
                         stop=True,
                     )
-                if j == 0 and (first == 0 or first >= 3 * PIECE):
+                if j == 0 and first in VECTOR_COPIES:
                     nc.vector.tensor_copy(out=key[:, first:last], in_=bank[:])
                 else:
                     nc.scalar.copy(out=key[:, first:last], in_=bank[:])
@@ -121,45 +125,42 @@ def tile_attend_grouppick_fresh_kernel(tc, emb_words, emb_scales, wk, query, off
         picked = sb.tile([P, PACK, I], F32, name="picked")
         for j in range(PACK - 1):
             nc.vector.tensor_copy(out=picked[:, j, :], in_=keys[j][:].indirect(offsets[:]))
-        for h in range(2):
+        for half in range(2):
+            columns = slice(half * I_HALF // LIST_ROWS, (half + 1) * I_HALF // LIST_ROWS)
             nc.vector.tensor_copy(
-                out=picked[:, PACK - 1, h * HALF : (h + 1) * HALF],
-                in_=keys[PACK - 1][:].indirect(offsets[:, h * (HALF // 16) : (h + 1) * (HALF // 16)]),
+                out=picked[:, PACK - 1, half * I_HALF : (half + 1) * I_HALF],
+                in_=keys[PACK - 1][:].indirect(offsets[:, columns]),
             )
 
-        QUARTER = I // 4
-        outer = [sb.tile([P, QUARTER * PACK], BF16, name="outer%d" % e, align_bytes=64) for e in range(2)]
-        middle = sb.tile([P, HALF * PACK], BF16, name="middle", tag="moving2", align_bytes=64)
-        woven = [outer[0][:], middle[:, 0 : QUARTER * PACK], middle[:, QUARTER * PACK : HALF * PACK], outer[1][:]]
+        outer = [sb.tile([P, I_QUARTER * PACK], BF16, name="outer%d" % e, align_bytes=64) for e in range(2)]
+        middle = sb.tile([P, I_HALF * PACK], BF16, name="middle", tag="emb1", align_bytes=64)
+        woven = [outer[0][:], middle[:, 0 : I_QUARTER * PACK], middle[:, I_QUARTER * PACK :], outer[1][:]]
 
-        def weave(copy, u):
-            copy(
+        def weave_whole(u):
+            nc.scalar.copy(
                 out=woven[u].rearrange("p (c i t) -> p c t i", i=4, t=PACK),
-                in_=picked[:, :, u * QUARTER : (u + 1) * QUARTER].rearrange("p t (c i) -> p c t i", i=4),
-            )
-
-        def weave_pair(copy, u, c):
-            copy(
-                out=woven[u].rearrange("p (i c t) -> p c i t", c=2, t=2)[:, c],
-                in_=picked[:, 2 * c : 2 * c + 2, u * QUARTER : (u + 1) * QUARTER].rearrange("p t i -> p i t"),
+                in_=picked[:, :, u * I_QUARTER : (u + 1) * I_QUARTER].rearrange("p t (c i) -> p c t i", i=4),
             )
 
         nc.scalar.copy(
             out=middle[:].rearrange("p (i c t) -> p c i t", c=2, t=2)[:, 0],
-            in_=picked[:, 0:2, QUARTER : I - QUARTER].rearrange("p t i -> p i t"),
+            in_=picked[:, 0:2, I_QUARTER : I - I_QUARTER].rearrange("p t i -> p i t"),
         )
-        weave(nc.scalar.copy, 0)
-        weave_pair(nc.vector.tensor_copy, 1, 1)
-        weave_pair(nc.vector.tensor_copy, 2, 1)
-        weave(nc.scalar.copy, 3)
+        weave_whole(0)
+        for u in (1, 2):
+            nc.vector.tensor_copy(
+                out=woven[u].rearrange("p (i c t) -> p c i t", c=2, t=2)[:, 1],
+                in_=picked[:, 2:4, u * I_QUARTER : (u + 1) * I_QUARTER].rearrange("p t i -> p i t"),
+            )
+        weave_whole(3)
 
         scores = score_ps.tile([P, I], F32, name="scores")
         for u in (1, 2, 0, 3):
-            k_codes = sb.tile([P, QUARTER], U32, name="k_codes%d" % u, align_bytes=64)
-            k_sc = sb.tile([P, QUARTER], U8, name="k_sc%d" % u, align_bytes=64)
+            k_codes = sb.tile([P, I_QUARTER], U32, name="k_codes%d" % u, align_bytes=64)
+            k_sc = sb.tile([P, I_QUARTER], U8, name="k_sc%d" % u, align_bytes=64)
             nc.vector.quantize_mx(out=k_codes[:].bitcast(FP8X4), scales=k_sc[:], in_=woven[u])
             nc.tensor.matmul_mx(
-                out=scores[:, u * QUARTER : (u + 1) * QUARTER],
+                out=scores[:, u * I_QUARTER : (u + 1) * I_QUARTER],
                 lhsT=q_codes[:].bitcast(FP8X4),
                 lhsT_scale=q_sc[:],
                 rhs=k_codes[:].bitcast(FP8X4),
@@ -167,19 +168,19 @@ def tile_attend_grouppick_fresh_kernel(tc, emb_words, emb_scales, wk, query, off
                 start=True,
                 stop=True,
             )
+
         neg_max = sb.tile([P, 1], F32, name="neg_max")
         nc.vector.tensor_reduce(out=neg_max[:], in_=scores[:], axis=mybir.AxisListType.X, op=ALU.max, negate=True)
-
         prob = sb.tile([P, I], F32, name="prob")
         total = sb.tile([P, 1], F32, name="total")
         nc.scalar.activation(prob[:], scores[:], EXP, bias=neg_max[:], scale=1.0, accum_out=total[:])
         inv = sb.tile([P, 1], F32, name="inv")
         nc.vector.reciprocal(inv[:], total[:])
-        for h in range(2):
-            cols = slice(h * HALF, (h + 1) * HALF)
-            res = sb.tile([P, HALF], F32, name="res%d" % h)
+
+        for half, queue in enumerate((nc.sync, nc.scalar)):
+            slots = slice(half * I_HALF, (half + 1) * I_HALF)
+            res = sb.tile([P, I_HALF], F32, name="res%d" % half)
             nc.vector.tensor_scalar(
-                out=res[:], in0=prob[:, cols], scalar1=inv[:], scalar2=float(I), op0=ALU.mult, op1=ALU.mult
+                out=res[:], in0=prob[:, slots], scalar1=inv[:], scalar2=float(I), op0=ALU.mult, op1=ALU.mult
             )
-            queue = nc.sync if h == 0 else nc.scalar
-            queue.dma_start(out=out[:, cols], in_=res[:])
+            queue.dma_start(out=out[:, slots], in_=res[:])

@@ -53,8 +53,8 @@ def tile_attend_grouppick_fresh_kernel(tc, emb_words, emb_scales, wk, query, off
             nc.sync.dma_start(out=raw[:], in_=wk_rows[:, 2 * pair : 2 * pair + 2, :])
             wk_raw.append(raw)
 
-        for g in range(4):
-            nc.sync.dma_start(
+        for g, queue in enumerate((nc.scalar, nc.scalar, nc.sync, nc.sync)):
+            queue.dma_start(
                 out=emb_sc[32 * g : 32 * g + 16, :].bitcast(I32),
                 in_=emb_scales[0, 4 * g : 4 * g + 4, :].bitcast(I32).rearrange("r (c n) -> c r n", c=4),
             )

@@ -29,9 +29,10 @@ PLANE_CUTS = [
     QUARTER_CUTS[:-1] + [T - P, T],
     QUARTER_CUTS,
     QUARTER_CUTS,
-    [0] + QUARTER_CUTS[2:],
+    QUARTER_CUTS,
 ]
-VECTOR_COPIES = (0, 2 * T_QUARTER)
+Q_LATE = 32
+VECTOR_COPIES = ((0, 0), (0, 2 * T_QUARTER), (3, 2 * T_QUARTER))
 
 
 def tile_attend_grouppick_fresh_kernel(tc, emb_words, emb_scales, wk, query, offs, out):
@@ -93,7 +94,7 @@ def tile_attend_grouppick_fresh_kernel(tc, emb_words, emb_scales, wk, query, off
             wk_codes = sb.tile([P, P], U32, name="wk_codes%d" % j, tag="stationary%d" % j, align_bytes=64)
             wk_sc = sb.tile([P, P], U8, name="wk_sc%d" % j, align_bytes=64)
             nc.vector.quantize_mx(out=wk_codes[:].bitcast(FP8X4), scales=wk_sc[:], in_=wk_bf[j][:])
-            key = sb.tile([P, T], F32, name="key%d" % j)
+            key = sb.tile([P, T], F32, name="key%d" % j, align_bytes=64)
             for first, last in zip(PLANE_CUTS[j], PLANE_CUTS[j][1:]):
                 bank = key_ps.tile([P, last - first], F32, name="key_bank")
                 for a in range(first, last, T_QUARTER):
@@ -107,58 +108,45 @@ def tile_attend_grouppick_fresh_kernel(tc, emb_words, emb_scales, wk, query, off
                         start=True,
                         stop=True,
                     )
-                if j == 0 and first in VECTOR_COPIES:
+                if (j, first) in VECTOR_COPIES:
                     nc.vector.tensor_copy(out=key[:, first:last], in_=bank[:])
                 else:
                     nc.scalar.copy(out=key[:, first:last], in_=bank[:])
             keys.append(key)
 
-        q_bf = sb.tile([P, Q * PACK], BF16, name="q_bf", tag="stationary%d" % (PACK - 1), align_bytes=64)
-        nc.scalar.copy(
-            out=q_bf[:].rearrange("p (c i t) -> p c t i", i=4, t=PACK),
-            in_=q_raw[:].rearrange("p (t c i) -> p c t i", i=4, t=PACK),
-        )
+        q_bf = sb.tile([P, Q * PACK], BF16, name="q_bf", tag="stationary1", align_bytes=64)
+        q_dst = q_bf[:].rearrange("p (c i t) -> p c t i", i=4, t=PACK)
+        q_src = q_raw[:].rearrange("p (t c i) -> p c t i", i=4, t=PACK)
+        early = (Q - Q_LATE) // 4
+        nc.vector.tensor_copy(out=q_dst[:, :early], in_=q_src[:, :early])
+        nc.scalar.copy(out=q_dst[:, early:], in_=q_src[:, early:])
+
+        picked = sb.tile([P, PACK, I], F32, name="picked")
+        for j in range(2):
+            nc.vector.tensor_copy(out=picked[:, j, :], in_=keys[j][:].indirect(offsets[:]))
+        for j in range(2, PACK):
+            columns = I_HALF // LIST_ROWS
+            nc.vector.tensor_copy(out=picked[:, j, :I_HALF], in_=keys[j][:].indirect(offsets[:, :columns]))
+            nc.scalar.activation(picked[:, j, I_HALF:], keys[j][:].indirect(offsets[:, columns:]), COPY)
+
         q_codes = sb.tile([P, Q], U32, name="q_codes", align_bytes=64)
         q_sc = sb.tile([P, Q], U8, name="q_sc", align_bytes=64)
         nc.vector.quantize_mx(out=q_codes[:].bitcast(FP8X4), scales=q_sc[:], in_=q_bf[:])
 
-        picked = sb.tile([P, PACK, I], F32, name="picked")
-        for j in range(PACK - 1):
-            nc.vector.tensor_copy(out=picked[:, j, :], in_=keys[j][:].indirect(offsets[:]))
-        for half in range(2):
-            columns = slice(half * I_HALF // LIST_ROWS, (half + 1) * I_HALF // LIST_ROWS)
-            nc.vector.tensor_copy(
-                out=picked[:, PACK - 1, half * I_HALF : (half + 1) * I_HALF],
-                in_=keys[PACK - 1][:].indirect(offsets[:, columns]),
-            )
-
-        outer = [sb.tile([P, I_QUARTER * PACK], BF16, name="outer%d" % e, align_bytes=64) for e in range(2)]
-        middle = sb.tile([P, I_HALF * PACK], BF16, name="middle", tag="emb1", align_bytes=64)
-        woven = [outer[0][:], middle[:, 0 : I_QUARTER * PACK], middle[:, I_QUARTER * PACK :], outer[1][:]]
-
-        def weave_whole(u):
-            nc.scalar.copy(
-                out=woven[u].rearrange("p (c i t) -> p c t i", i=4, t=PACK),
-                in_=picked[:, :, u * I_QUARTER : (u + 1) * I_QUARTER].rearrange("p t (c i) -> p c t i", i=4),
-            )
-
-        nc.scalar.copy(
-            out=middle[:].rearrange("p (i c t) -> p c i t", c=2, t=2)[:, 0],
-            in_=picked[:, 0:2, I_QUARTER : I - I_QUARTER].rearrange("p t i -> p i t"),
-        )
-        weave_whole(0)
-        for u in (1, 2):
-            nc.vector.tensor_copy(
-                out=woven[u].rearrange("p (i c t) -> p c i t", c=2, t=2)[:, 1],
-                in_=picked[:, 2:4, u * I_QUARTER : (u + 1) * I_QUARTER].rearrange("p t i -> p i t"),
-            )
-        weave_whole(3)
+        woven = [sb.tile([P, I_QUARTER * PACK], BF16, name="woven%d" % u, align_bytes=64) for u in range(4)]
+        for u in range(4):
+            dst = woven[u][:].rearrange("p (c i t) -> p c t i", i=4, t=PACK)
+            src = picked[:, :, u * I_QUARTER : (u + 1) * I_QUARTER].rearrange("p t (c i) -> p c t i", i=4)
+            if u >= 2:
+                nc.vector.tensor_copy(out=dst, in_=src)
+            else:
+                nc.scalar.copy(out=dst, in_=src)
 
         scores = score_ps.tile([P, I], F32, name="scores")
-        for u in (1, 2, 0, 3):
+        for u in (2, 3, 0, 1):
             k_codes = sb.tile([P, I_QUARTER], U32, name="k_codes%d" % u, align_bytes=64)
             k_sc = sb.tile([P, I_QUARTER], U8, name="k_sc%d" % u, align_bytes=64)
-            nc.vector.quantize_mx(out=k_codes[:].bitcast(FP8X4), scales=k_sc[:], in_=woven[u])
+            nc.vector.quantize_mx(out=k_codes[:].bitcast(FP8X4), scales=k_sc[:], in_=woven[u][:])
             nc.tensor.matmul_mx(
                 out=scores[:, u * I_QUARTER : (u + 1) * I_QUARTER],
                 lhsT=q_codes[:].bitcast(FP8X4),

@@ -26,13 +26,14 @@ I_QUARTER = I // 4
 
 QUARTER_CUTS = list(range(0, T + 1, T_QUARTER))
 PLANE_CUTS = [
-    QUARTER_CUTS[:-1] + [T - P, T],
-    QUARTER_CUTS,
-    QUARTER_CUTS,
-    QUARTER_CUTS,
+    [0, 256, 512, 768, 896, 1024],
+    [0, 256, 512, 768, 1024],
+    [0, 256, 512, 768, 1024],
+    [0, 256, 512, 768, 1024],
 ]
-Q_LATE = 32
-VECTOR_COPIES = ((0, 0), (0, 2 * T_QUARTER), (3, 2 * T_QUARTER))
+VECTOR_COPIES = ((0, 0), (0, 512), (3, 512),)
+WEAVES = (("scalar", 0, 128), ("scalar", 128, 256), ("vector", 256, 384), ("vector", 384, 512),)
+PASSES = ((256, 384), (384, 512), (0, 128), (128, 256),)
 
 
 def tile_attend_grouppick_fresh_kernel(tc, emb_words, emb_scales, wk, query, offs, out):
@@ -114,12 +115,15 @@ def tile_attend_grouppick_fresh_kernel(tc, emb_words, emb_scales, wk, query, off
                     nc.scalar.copy(out=key[:, first:last], in_=bank[:])
             keys.append(key)
 
-        q_bf = sb.tile([P, Q * PACK], BF16, name="q_bf", tag="stationary1", align_bytes=64)
-        q_dst = q_bf[:].rearrange("p (c i t) -> p c t i", i=4, t=PACK)
-        q_src = q_raw[:].rearrange("p (t c i) -> p c t i", i=4, t=PACK)
-        early = (Q - Q_LATE) // 4
-        nc.vector.tensor_copy(out=q_dst[:, :early], in_=q_src[:, :early])
-        nc.scalar.copy(out=q_dst[:, early:], in_=q_src[:, early:])
+        q_bf = sb.tile([P, Q * PACK], BF16, name="q_bf", align_bytes=64)
+        nc.gpsimd.tensor_scalar(
+            out=q_bf[:].rearrange("p (i t) -> p i t", t=PACK),
+            in0=q_raw[:].rearrange("p (t i) -> p i t", t=PACK),
+            scalar1=1.0,
+            scalar2=0.0,
+            op0=ALU.mult,
+            op1=ALU.add,
+        )
 
         picked = sb.tile([P, PACK, I], F32, name="picked")
         for j in range(2):
@@ -129,26 +133,34 @@ def tile_attend_grouppick_fresh_kernel(tc, emb_words, emb_scales, wk, query, off
             nc.vector.tensor_copy(out=picked[:, j, :I_HALF], in_=keys[j][:].indirect(offsets[:, :columns]))
             nc.scalar.activation(picked[:, j, I_HALF:], keys[j][:].indirect(offsets[:, columns:]), COPY)
 
-        q_codes = sb.tile([P, Q], U32, name="q_codes", align_bytes=64)
+        q_codes = sb.tile([P, Q], U32, name="q_codes", tag="stationary3", align_bytes=64)
         q_sc = sb.tile([P, Q], U8, name="q_sc", align_bytes=64)
         nc.vector.quantize_mx(out=q_codes[:].bitcast(FP8X4), scales=q_sc[:], in_=q_bf[:])
 
-        woven = [sb.tile([P, I_QUARTER * PACK], BF16, name="woven%d" % u, align_bytes=64) for u in range(4)]
-        for u in range(4):
-            dst = woven[u][:].rearrange("p (c i t) -> p c t i", i=4, t=PACK)
-            src = picked[:, :, u * I_QUARTER : (u + 1) * I_QUARTER].rearrange("p t (c i) -> p c t i", i=4)
-            if u >= 2:
+        woven = {}
+        for engine, first, last in WEAVES:
+            tile = sb.tile([P, (last - first) * PACK], BF16, name="woven%d" % first, align_bytes=64)
+            dst = tile[:].rearrange("p (c i t) -> p c t i", i=4, t=PACK)
+            src = picked[:, :, first:last].rearrange("p t (c i) -> p c t i", i=4)
+            if engine == "vector":
                 nc.vector.tensor_copy(out=dst, in_=src)
             else:
                 nc.scalar.copy(out=dst, in_=src)
+            for slot in range(first, last, 64):
+                woven[slot] = (tile, first)
 
         scores = score_ps.tile([P, I], F32, name="scores")
-        for u in (2, 3, 0, 1):
-            k_codes = sb.tile([P, I_QUARTER], U32, name="k_codes%d" % u, align_bytes=64)
-            k_sc = sb.tile([P, I_QUARTER], U8, name="k_sc%d" % u, align_bytes=64)
-            nc.vector.quantize_mx(out=k_codes[:].bitcast(FP8X4), scales=k_sc[:], in_=woven[u][:])
+        for first, last in PASSES:
+            tile, start = woven[first]
+            k_codes = sb.tile([P, last - first], U32, name="k_codes%d" % first, align_bytes=64)
+            k_sc = sb.tile([P, last - first], U8, name="k_sc%d" % first, align_bytes=64)
+            nc.vector.quantize_mx(
+                out=k_codes[:].bitcast(FP8X4),
+                scales=k_sc[:],
+                in_=tile[:, (first - start) * PACK : (last - start) * PACK],
+            )
             nc.tensor.matmul_mx(
-                out=scores[:, u * I_QUARTER : (u + 1) * I_QUARTER],
+                out=scores[:, first:last],
                 lhsT=q_codes[:].bitcast(FP8X4),
                 lhsT_scale=q_sc[:],
                 rhs=k_codes[:].bitcast(FP8X4),

@@ -33,7 +33,7 @@ PLANE_CUTS = [
 ]
 VECTOR_COPIES = ((0, 0), (0, 512), (3, 512),)
 WEAVES = (("scalar", 0, 128), ("scalar", 128, 256), ("vector", 256, 384), ("vector", 384, 512),)
-PASSES = ((256, 384), (384, 512), (0, 128), (128, 256),)
+PASSES = ((256, 384), (0, 128), (384, 512), (128, 256),)
 
 
 def tile_attend_grouppick_fresh_kernel(tc, emb_words, emb_scales, wk, query, offs, out):
@@ -73,7 +73,7 @@ def tile_attend_grouppick_fresh_kernel(tc, emb_words, emb_scales, wk, query, off
 
         nc.sync.dma_start(offsets[:], offs)
 
-        q_raw = sb.tile([P, PACK * Q], F32, name="q_raw")
+        q_raw = sb.tile([P, PACK * Q], F32, name="q_raw", align_bytes=64)
         q_planes = query.rearrange("(b j r) q -> j b r q", j=PACK, r=8)
         for j in range(PACK):
             nc.sync.dma_start(out=q_raw[:, j * Q : (j + 1) * Q], in_=q_planes[j])
@@ -138,16 +138,30 @@ def tile_attend_grouppick_fresh_kernel(tc, emb_words, emb_scales, wk, query, off
         nc.vector.quantize_mx(out=q_codes[:].bitcast(FP8X4), scales=q_sc[:], in_=q_bf[:])
 
         woven = {}
+        ahead = sb.tile([P, I_HALF * PACK], BF16, name="ahead", tag="q_raw", align_bytes=64)
+        pairs = ahead[:].rearrange("p (i c t) -> p c i t", c=2, t=2)
+        nc.gpsimd.tensor_scalar(
+            out=pairs[:, 0],
+            in0=picked[:, 0:2, :I_HALF].rearrange("p t i -> p i t"),
+            scalar1=1.0,
+            scalar2=0.0,
+            op0=ALU.mult,
+            op1=ALU.add,
+        )
         for engine, first, last in WEAVES:
-            tile = sb.tile([P, (last - first) * PACK], BF16, name="woven%d" % first, align_bytes=64)
-            dst = tile[:].rearrange("p (c i t) -> p c t i", i=4, t=PACK)
-            src = picked[:, :, first:last].rearrange("p t (c i) -> p c t i", i=4)
             if engine == "vector":
-                nc.vector.tensor_copy(out=dst, in_=src)
+                tile = sb.tile([P, (last - first) * PACK], BF16, name="woven%d" % first, align_bytes=64)
+                nc.vector.tensor_copy(
+                    out=tile[:].rearrange("p (c i t) -> p c t i", i=4, t=PACK),
+                    in_=picked[:, :, first:last].rearrange("p t (c i) -> p c t i", i=4),
+                )
+                woven[first] = (tile, first)
             else:
-                nc.scalar.copy(out=dst, in_=src)
-            for slot in range(first, last, 64):
-                woven[slot] = (tile, first)
+                nc.scalar.copy(
+                    out=pairs[:, 1, first:last],
+                    in_=picked[:, 2:4, first:last].rearrange("p t i -> p i t"),
+                )
+                woven[first] = (ahead, 0)
 
         scores = score_ps.tile([P, I], F32, name="scores")
         for first, last in PASSES:

@@ -26,14 +26,14 @@ I_QUARTER = I // 4
 
 QUARTER_CUTS = list(range(0, T + 1, T_QUARTER))
 PLANE_CUTS = [
-    [0, 256, 512, 768, 896, 1024],
+    [0, 256, 512, 640, 768, 896, 1024],
     [0, 256, 512, 768, 1024],
     [0, 256, 512, 768, 1024],
     [0, 256, 512, 768, 1024],
 ]
 VECTOR_COPIES = ((0, 0), (0, 512), (3, 512),)
-WEAVES = (("scalar", 0, 128), ("scalar", 128, 256), ("vector", 256, 384), ("vector", 384, 512),)
-PASSES = ((256, 384), (0, 128), (384, 512), (128, 256),)
+WEAVES = (("scalar", 0, 128), ("scalar", 128, 256), ("vector", 384, 512), ("vector", 256, 384),)
+PASSES = ((384, 512), (0, 128), (256, 384), (128, 256),)
 
 
 def tile_attend_grouppick_fresh_kernel(tc, emb_words, emb_scales, wk, query, offs, out):
@@ -126,28 +126,44 @@ def tile_attend_grouppick_fresh_kernel(tc, emb_words, emb_scales, wk, query, off
         )
 
         picked = sb.tile([P, PACK, I], F32, name="picked")
+        quarter = I_QUARTER // LIST_ROWS
+
+        def gather_quarter(j, u, row):
+            nc.vector.tensor_copy(
+                out=picked[:, row, u * I_QUARTER : (u + 1) * I_QUARTER].bitcast(U32),
+                in_=keys[j][:].bitcast(U32).indirect(offsets[:, u * quarter : (u + 1) * quarter]),
+            )
+
         for j in range(2):
             nc.vector.tensor_copy(out=picked[:, j, :], in_=keys[j][:].indirect(offsets[:]))
-        for j in range(2, PACK):
-            columns = I_HALF // LIST_ROWS
-            nc.vector.tensor_copy(out=picked[:, j, :I_HALF], in_=keys[j][:].indirect(offsets[:, :columns]))
-            nc.scalar.activation(picked[:, j, I_HALF:], keys[j][:].indirect(offsets[:, columns:]), COPY)
+        ahead = sb.tile([P, I_HALF * PACK], BF16, name="ahead", tag="q_raw", align_bytes=64)
+        pairs = ahead[:].rearrange("p (i c t) -> p c i t", c=2, t=2)
+        for u in (1, 0):
+            slots = slice(u * I_QUARTER, (u + 1) * I_QUARTER)
+            nc.gpsimd.tensor_scalar(
+                out=pairs[:, 0, slots],
+                in0=picked[:, 0:2, slots].rearrange("p t i -> p i t"),
+                scalar1=1.0,
+                scalar2=0.0,
+                op0=ALU.mult,
+                op1=ALU.add,
+            )
+        gather_quarter(2, 0, 2)
+        gather_quarter(3, 3, 3)
+        gather_quarter(3, 0, 3)
+        gather_quarter(2, 1, 1)
+        for j, u in ((2, 2), (3, 1)):
+            nc.scalar.activation(
+                picked[:, j, u * I_QUARTER : (u + 2) * I_QUARTER],
+                keys[j][:].indirect(offsets[:, u * quarter : (u + 2) * quarter]),
+                COPY,
+            )
 
         q_codes = sb.tile([P, Q], U32, name="q_codes", tag="stationary3", align_bytes=64)
         q_sc = sb.tile([P, Q], U8, name="q_sc", align_bytes=64)
         nc.vector.quantize_mx(out=q_codes[:].bitcast(FP8X4), scales=q_sc[:], in_=q_bf[:])
 
         woven = {}
-        ahead = sb.tile([P, I_HALF * PACK], BF16, name="ahead", tag="q_raw", align_bytes=64)
-        pairs = ahead[:].rearrange("p (i c t) -> p c i t", c=2, t=2)
-        nc.gpsimd.tensor_scalar(
-            out=pairs[:, 0],
-            in0=picked[:, 0:2, :I_HALF].rearrange("p t i -> p i t"),
-            scalar1=1.0,
-            scalar2=0.0,
-            op0=ALU.mult,
-            op1=ALU.add,
-        )
         for engine, first, last in WEAVES:
             if engine == "vector":
                 tile = sb.tile([P, (last - first) * PACK], BF16, name="woven%d" % first, align_bytes=64)
@@ -157,9 +173,10 @@ def tile_attend_grouppick_fresh_kernel(tc, emb_words, emb_scales, wk, query, off
                 )
                 woven[first] = (tile, first)
             else:
+                rows = slice(2, 4) if first == 0 else slice(1, 4, 2)
                 nc.scalar.copy(
                     out=pairs[:, 1, first:last],
-                    in_=picked[:, 2:4, first:last].rearrange("p t i -> p i t"),
+                    in_=picked[:, rows, first:last].rearrange("p t i -> p i t"),
                 )
                 woven[first] = (ahead, 0)
 

@@ -134,8 +134,12 @@ def tile_attend_grouppick_fresh_kernel(tc, emb_words, emb_scales, wk, query, off
                 in_=keys[j][:].bitcast(U32).indirect(offsets[:, u * quarter : (u + 1) * quarter]),
             )
 
-        for j in range(2):
-            nc.vector.tensor_copy(out=picked[:, j, :], in_=keys[j][:].indirect(offsets[:]))
+        nc.vector.tensor_copy(out=picked[:, 0, :], in_=keys[0][:].indirect(offsets[:]))
+        for half in range(2):
+            nc.vector.tensor_copy(
+                out=picked[:, 1, half * I_HALF : (half + 1) * I_HALF],
+                in_=keys[1][:].indirect(offsets[:, 2 * half * quarter : 2 * (half + 1) * quarter]),
+            )
         ahead = sb.tile([P, I_HALF * PACK], BF16, name="ahead", tag="q_raw", align_bytes=64)
         pairs = ahead[:].rearrange("p (i c t) -> p c i t", c=2, t=2)
         for u in (1, 0):

@@ -184,7 +184,11 @@ def tile_attend_grouppick_fresh_kernel(tc, emb_words, emb_scales, wk, query, off
                 )
                 woven[first] = (ahead, 0)
 
-        scores = score_ps.tile([P, I], F32, name="scores")
+        early, late = slice(384, 512), slice(0, 384)
+        banks = [
+            key_ps.tile([P, early.stop - early.start], F32, name="scores_early", tag="key_bank"),
+            score_ps.tile([P, late.stop - late.start], F32, name="scores_late"),
+        ]
         for first, last in PASSES:
             tile, start = woven[first]
             k_codes = sb.tile([P, last - first], U32, name="k_codes%d" % first, align_bytes=64)
@@ -195,7 +199,11 @@ def tile_attend_grouppick_fresh_kernel(tc, emb_words, emb_scales, wk, query, off
                 in_=tile[:, (first - start) * PACK : (last - start) * PACK],
             )
             nc.tensor.matmul_mx(
-                out=scores[:, first:last],
+                out=(
+                    banks[0][:, first - early.start : last - early.start]
+                    if early.start <= first < early.stop
+                    else banks[1][:, first - late.start : last - late.start]
+                ),
                 lhsT=q_codes[:].bitcast(FP8X4),
                 lhsT_scale=q_sc[:],
                 rhs=k_codes[:].bitcast(FP8X4),
@@ -204,11 +212,22 @@ def tile_attend_grouppick_fresh_kernel(tc, emb_words, emb_scales, wk, query, off
                 stop=True,
             )
 
+        neg = sb.tile([P, I], F32, name="neg")
+        neg_max_early = sb.tile([P, 1], F32, name="neg_max_early")
         neg_max = sb.tile([P, 1], F32, name="neg_max")
-        nc.vector.tensor_reduce(out=neg_max[:], in_=scores[:], axis=mybir.AxisListType.X, op=ALU.max, negate=True)
+        for bank, part, start, result in ((banks[0], early, None, neg_max_early), (banks[1], late, neg_max_early[:], neg_max)):
+            nc.vector.tensor_scalar(
+                out=neg[:, part],
+                in0=bank[:],
+                scalar1=-1.0,
+                scalar2=start,
+                op0=ALU.mult,
+                op1=ALU.min,
+                accum_out=result[:],
+            )
         prob = sb.tile([P, I], F32, name="prob")
         total = sb.tile([P, 1], F32, name="total")
-        nc.scalar.activation(prob[:], scores[:], EXP, bias=neg_max[:], scale=1.0, accum_out=total[:])
+        nc.scalar.activation(prob[:], neg[:], EXP, bias=neg_max[:], scale=-1.0, accum_out=total[:])
         inv = sb.tile([P, 1], F32, name="inv")
         nc.vector.reciprocal(inv[:], total[:])
 

@@ -31,7 +31,7 @@ PLANE_CUTS = [
     [0, 256, 512, 768, 1024],
     [0, 256, 512, 768, 1024],
 ]
-VECTOR_COPIES = ((0, 0), (0, 512), (3, 512),)
+VECTOR_COPIES = ((0, 0), (0, 512), (3, 768),)
 WEAVES = (("scalar", 0, 128), ("scalar", 128, 256), ("vector", 384, 512), ("vector", 256, 384),)
 PASSES = ((384, 512), (0, 128), (256, 384), (128, 256),)
 
@@ -40,8 +40,7 @@ def tile_attend_grouppick_fresh_kernel(tc, emb_words, emb_scales, wk, query, off
     nc = tc.nc
     with ExitStack() as ctx:
         sb = ctx.enter_context(tc.tile_pool(name="sb", bufs=1))
-        key_ps = ctx.enter_context(tc.psum_pool(name="key_ps", bufs=7))
-        score_ps = ctx.enter_context(tc.psum_pool(name="score_ps", bufs=1))
+        key_ps = ctx.enter_context(tc.psum_pool(name="key_ps", bufs=8))
 
         offsets = sb.tile([P, I // LIST_ROWS], U16, name="offsets")
 
@@ -78,23 +77,34 @@ def tile_attend_grouppick_fresh_kernel(tc, emb_words, emb_scales, wk, query, off
         for j in range(PACK):
             nc.sync.dma_start(out=q_raw[:, j * Q : (j + 1) * Q], in_=q_planes[j])
 
-        wk_bf = [sb.tile([P, P * PACK], BF16, name="wk_bf%d" % j, align_bytes=64) for j in range(PACK)]
+        parts = [(0, 0, P // 2), (0, P // 2, P)] + [(j, 0, P) for j in range(1, PACK)]
+        wk_bf = [
+            sb.tile([P, (last - first) * PACK], BF16, name="wk_bf%d_%d" % (j, first), align_bytes=64)
+            for j, first, last in parts
+        ]
         for pair in range(2):
             src = wk_raw[pair][:].rearrange("p t (b j r) -> p j b r t", j=PACK, r=8)
-            for j in range(PACK):
-                dst = wk_bf[j][:].rearrange("p (b r c t) -> p c b r t", c=2, r=8, t=2)
-                if j < 2:
-                    nc.vector.tensor_copy(out=dst[:, pair], in_=src[:, j])
+            for tile, (j, first, last) in zip(wk_bf, parts):
+                dst = tile[:].rearrange("p (b r c t) -> p c b r t", c=2, r=8, t=2)[:, pair]
+                rows = src[:, j, first // 8 : last // 8]
+                if j == 0 or (j == 1 and pair == 0):
+                    nc.vector.tensor_copy(out=dst, in_=rows)
                 elif pair == 0:
-                    nc.scalar.activation(dst[:, pair], src[:, j], COPY)
+                    nc.scalar.activation(dst, rows, COPY)
                 else:
-                    nc.scalar.copy(out=dst[:, pair], in_=src[:, j])
+                    nc.scalar.copy(out=dst, in_=rows)
+
+        wk_codes = [
+            sb.tile([P, P], U32, name="wk_codes%d" % j, tag="stationary%d" % j, align_bytes=64) for j in range(PACK)
+        ]
+        wk_scales = [sb.tile([P, P], U8, name="wk_sc%d" % j, align_bytes=64) for j in range(PACK)]
+        for tile, (j, first, last) in zip(wk_bf, parts):
+            nc.vector.quantize_mx(
+                out=wk_codes[j][:, first:last].bitcast(FP8X4), scales=wk_scales[j][:, first:last], in_=tile[:]
+            )
 
         keys = []
         for j in range(PACK):
-            wk_codes = sb.tile([P, P], U32, name="wk_codes%d" % j, tag="stationary%d" % j, align_bytes=64)
-            wk_sc = sb.tile([P, P], U8, name="wk_sc%d" % j, align_bytes=64)
-            nc.vector.quantize_mx(out=wk_codes[:].bitcast(FP8X4), scales=wk_sc[:], in_=wk_bf[j][:])
             key = sb.tile([P, T], F32, name="key%d" % j, align_bytes=64)
             for first, last in zip(PLANE_CUTS[j], PLANE_CUTS[j][1:]):
                 bank = key_ps.tile([P, last - first], F32, name="key_bank")
@@ -102,8 +112,8 @@ def tile_attend_grouppick_fresh_kernel(tc, emb_words, emb_scales, wk, query, off
                     width = min(T_QUARTER, last - a)
                     nc.tensor.matmul_mx(
                         out=bank[:, a - first : a - first + width],
-                        lhsT=wk_codes[:].bitcast(FP8X4),
-                        lhsT_scale=wk_sc[:],
+                        lhsT=wk_codes[j][:].bitcast(FP8X4),
+                        lhsT_scale=wk_scales[j][:],
                         rhs=emb_codes[a // T_HALF][:, a % T_HALF : a % T_HALF + width].bitcast(FP8X4),
                         rhs_scale=emb_sc[4 * (a // T_QUARTER) :, a % T_QUARTER : a % T_QUARTER + width],
                         start=True,
@@ -187,7 +197,7 @@ def tile_attend_grouppick_fresh_kernel(tc, emb_words, emb_scales, wk, query, off
         early, late = slice(384, 512), slice(0, 384)
         banks = [
             key_ps.tile([P, early.stop - early.start], F32, name="scores_early", tag="key_bank"),
-            score_ps.tile([P, late.stop - late.start], F32, name="scores_late"),
+            key_ps.tile([P, late.stop - late.start], F32, name="scores_late", tag="key_bank"),
         ]
         for first, last in PASSES:
             tile, start = woven[first]

@@ -22,6 +22,7 @@ LIST_ROWS = 16
 T_HALF = T // 2
 T_QUARTER = T // 4
 I_HALF = I // 2
+WARM_ROWS = 32
 I_QUARTER = I // 4
 
 QUARTER_CUTS = list(range(0, T + 1, T_QUARTER))
@@ -176,6 +177,18 @@ def tile_attend_grouppick_fresh_kernel(tc, emb_words, emb_scales, wk, query, off
         q_codes = sb.tile([P, Q], U32, name="q_codes", tag="stationary3", align_bytes=64)
         q_sc = sb.tile([P, Q], U8, name="q_sc", align_bytes=64)
         nc.vector.quantize_mx(out=q_codes[:].bitcast(FP8X4), scales=q_sc[:], in_=q_bf[:])
+
+        warm_bank = key_ps.tile([WARM_ROWS, T_HALF], F32, name="warm_bank", tag="key_bank")
+        for half in range(3):
+            nc.tensor.matmul_mx(
+                out=warm_bank[:],
+                lhsT=q_codes[:, :WARM_ROWS].bitcast(FP8X4),
+                lhsT_scale=q_sc[:, :WARM_ROWS],
+                rhs=emb_codes[half % 2][:].bitcast(FP8X4),
+                rhs_scale=emb_codes[half % 2][:].bitcast(U8)[:, :T_HALF],
+                start=True,
+                stop=True,
+            )
 
         woven = {}
         for engine, first, last in WEAVES:

@@ -254,10 +254,8 @@ def tile_attend_grouppick_fresh_kernel(tc, emb_words, emb_scales, wk, query, off
         inv = sb.tile([P, 1], F32, name="inv")
         nc.vector.reciprocal(inv[:], total[:])
 
-        for half, queue in enumerate((nc.sync, nc.scalar)):
-            slots = slice(half * I_HALF, (half + 1) * I_HALF)
-            res = sb.tile([P, I_HALF], F32, name="res%d" % half)
-            nc.vector.tensor_scalar(
-                out=res[:], in0=prob[:, slots], scalar1=inv[:], scalar2=float(I), op0=ALU.mult, op1=ALU.mult
-            )
-            queue.dma_start(out=out[:, slots], in_=res[:])
+        res = sb.tile([P, I], F32, name="res")
+        nc.vector.tensor_scalar(
+            out=res[:], in0=prob[:], scalar1=inv[:], scalar2=float(I), op0=ALU.mult, op1=ALU.mult
+        )
+        nc.sync.dma_start(out=out, in_=res[:])

@@ -21,30 +21,25 @@ PACK = 4
 LIST_ROWS = 16
 T_HALF = T // 2
 T_QUARTER = T // 4
-I_HALF = I // 2
-WARM_ROWS = 32
 I_QUARTER = I // 4
 
-QUARTER_CUTS = list(range(0, T + 1, T_QUARTER))
 PLANE_CUTS = [
     [0, 256, 512, 640, 768, 896, 1024],
     [0, 256, 512, 768, 1024],
-    [0, 256, 512, 768, 1024],
-    [0, 256, 512, 768, 1024],
+    [0, 512, 1024],
+    [0, 512, 1024],
 ]
-VECTOR_COPIES = ((0, 0), (0, 512), (3, 768),)
-WEAVES = (("scalar", 0, 128), ("scalar", 128, 256), ("vector", 384, 512), ("vector", 256, 384),)
-PASSES = ((384, 512), (0, 128), (256, 384), (128, 256),)
+SCALAR_COPIES = ((0, 256), (0, 512), (0, 640), (0, 768), (3, 512))
+PASSES = (3, 0, 2, 1)
 
 
 def tile_attend_grouppick_fresh_kernel(tc, emb_words, emb_scales, wk, query, offs, out):
     nc = tc.nc
     with ExitStack() as ctx:
         sb = ctx.enter_context(tc.tile_pool(name="sb", bufs=1))
-        key_ps = ctx.enter_context(tc.psum_pool(name="key_ps", bufs=8))
+        ps = ctx.enter_context(tc.psum_pool(name="ps", bufs=8))
 
         offsets = sb.tile([P, I // LIST_ROWS], U16, name="offsets")
-
         emb_sc = sb.tile([P, T_QUARTER], U8, name="emb_sc", align_bytes=64)
         nc.vector.memset(emb_sc[:].bitcast(I32), 0)
 
@@ -54,25 +49,21 @@ def tile_attend_grouppick_fresh_kernel(tc, emb_words, emb_scales, wk, query, off
             raw = sb.tile([P, 2, D], F32, name="wk_raw%d" % pair)
             nc.sync.dma_start(out=raw[:], in_=wk_rows[:, 2 * pair : 2 * pair + 2, :])
             wk_raw.append(raw)
-
         for g, queue in enumerate((nc.scalar, nc.scalar, nc.sync, nc.sync)):
             queue.dma_start(
                 out=emb_sc[32 * g : 32 * g + 16, :].bitcast(I32),
                 in_=emb_scales[0, 4 * g : 4 * g + 4, :].bitcast(I32).rearrange("r (c n) -> c r n", c=4),
             )
-
         emb_bytes = emb_words[0].rearrange("p n t -> p (n t)")
         emb_codes = []
         for half in range(2):
-            codes = sb.tile([P, T_HALF], U32, name="emb_codes%d" % half, tag="emb%d" % half, align_bytes=64)
+            codes = sb.tile([P, T_HALF], U32, name="emb_codes%d" % half, align_bytes=64)
             nc.sync.dma_start(
                 out=codes[:].bitcast(I32),
                 in_=emb_bytes[:, half * T_HALF * PACK : (half + 1) * T_HALF * PACK].bitcast(I32),
             )
             emb_codes.append(codes)
-
         nc.sync.dma_start(offsets[:], offs)
-
         q_raw = sb.tile([P, PACK * Q], F32, name="q_raw", align_bytes=64)
         q_planes = query.rearrange("(b j r) q -> j b r q", j=PACK, r=8)
         for j in range(PACK):
@@ -104,13 +95,30 @@ def tile_attend_grouppick_fresh_kernel(tc, emb_words, emb_scales, wk, query, off
                 out=wk_codes[j][:, first:last].bitcast(FP8X4), scales=wk_scales[j][:, first:last], in_=tile[:]
             )
 
+        picked = sb.tile([P, PACK, I], F32, name="picked")
+        quarter = I_QUARTER // LIST_ROWS
         keys = []
+
+        def gather_scalar(j, first, last):
+            nc.scalar.activation(
+                picked[:, j, first * I_QUARTER : last * I_QUARTER],
+                keys[j][:].indirect(offsets[:, first * quarter : last * quarter]),
+                COPY,
+            )
+
+        def gather_vector(j, first, last):
+            nc.vector.tensor_copy(
+                out=picked[:, j, first * I_QUARTER : last * I_QUARTER].bitcast(U32),
+                in_=keys[j][:].bitcast(U32).indirect(offsets[:, first * quarter : last * quarter]),
+            )
+
         for j in range(PACK):
-            key = sb.tile([P, T], F32, name="key%d" % j, align_bytes=64)
+            key = sb.tile([P, T], F32, name="key%d" % j, tag="key%d" % j, align_bytes=64)
             for first, last in zip(PLANE_CUTS[j], PLANE_CUTS[j][1:]):
-                bank = key_ps.tile([P, last - first], F32, name="key_bank")
-                for a in range(first, last, T_QUARTER):
-                    width = min(T_QUARTER, last - a)
+                bank = ps.tile([P, last - first], F32, name="bank")
+                starts = [first] + list(range(first // T_QUARTER * T_QUARTER + T_QUARTER, last, T_QUARTER))
+                for a, end in zip(starts, starts[1:] + [last]):
+                    width = end - a
                     nc.tensor.matmul_mx(
                         out=bank[:, a - first : a - first + width],
                         lhsT=wk_codes[j][:].bitcast(FP8X4),
@@ -120,11 +128,15 @@ def tile_attend_grouppick_fresh_kernel(tc, emb_words, emb_scales, wk, query, off
                         start=True,
                         stop=True,
                     )
-                if (j, first) in VECTOR_COPIES:
-                    nc.vector.tensor_copy(out=key[:, first:last], in_=bank[:])
-                else:
+                if (j, first) in SCALAR_COPIES:
                     nc.scalar.copy(out=key[:, first:last], in_=bank[:])
+                else:
+                    nc.vector.tensor_copy(out=key[:, first:last], in_=bank[:])
             keys.append(key)
+            if j == 0:
+                gather_scalar(0, 0, 4)
+            if j == 1:
+                gather_scalar(1, 0, 4)
 
         q_bf = sb.tile([P, Q * PACK], BF16, name="q_bf", align_bytes=64)
         nc.gpsimd.tensor_scalar(
@@ -135,98 +147,48 @@ def tile_attend_grouppick_fresh_kernel(tc, emb_words, emb_scales, wk, query, off
             op0=ALU.mult,
             op1=ALU.add,
         )
-
-        picked = sb.tile([P, PACK, I], F32, name="picked")
-        quarter = I_QUARTER // LIST_ROWS
-
-        def gather_quarter(j, u, row):
-            nc.vector.tensor_copy(
-                out=picked[:, row, u * I_QUARTER : (u + 1) * I_QUARTER].bitcast(U32),
-                in_=keys[j][:].bitcast(U32).indirect(offsets[:, u * quarter : (u + 1) * quarter]),
-            )
-
-        nc.vector.tensor_copy(out=picked[:, 0, :], in_=keys[0][:].indirect(offsets[:]))
-        for half in range(2):
-            nc.vector.tensor_copy(
-                out=picked[:, 1, half * I_HALF : (half + 1) * I_HALF],
-                in_=keys[1][:].indirect(offsets[:, 2 * half * quarter : 2 * (half + 1) * quarter]),
-            )
-        ahead = sb.tile([P, I_HALF * PACK], BF16, name="ahead", tag="q_raw", align_bytes=64)
+        ahead = sb.tile([P, 2 * I_QUARTER * PACK], BF16, name="ahead", tag="q_raw", align_bytes=64)
         pairs = ahead[:].rearrange("p (i c t) -> p c i t", c=2, t=2)
-        for u in (1, 0):
-            slots = slice(u * I_QUARTER, (u + 1) * I_QUARTER)
-            nc.gpsimd.tensor_scalar(
-                out=pairs[:, 0, slots],
-                in0=picked[:, 0:2, slots].rearrange("p t i -> p i t"),
-                scalar1=1.0,
-                scalar2=0.0,
-                op0=ALU.mult,
-                op1=ALU.add,
-            )
-        gather_quarter(2, 0, 2)
-        gather_quarter(3, 3, 3)
-        gather_quarter(3, 0, 3)
-        gather_quarter(2, 1, 1)
-        for j, u in ((2, 2), (3, 1)):
-            nc.scalar.activation(
-                picked[:, j, u * I_QUARTER : (u + 2) * I_QUARTER],
-                keys[j][:].indirect(offsets[:, u * quarter : (u + 2) * quarter]),
-                COPY,
-            )
+        nc.gpsimd.tensor_scalar(
+            out=pairs[:, 0],
+            in0=picked[:, 0:2, : 2 * I_QUARTER].rearrange("p t i -> p i t"),
+            scalar1=1.0,
+            scalar2=0.0,
+            op0=ALU.mult,
+            op1=ALU.add,
+        )
 
-        q_codes = sb.tile([P, Q], U32, name="q_codes", tag="stationary3", align_bytes=64)
+        gather_scalar(2, 2, 4)
+        gather_scalar(3, 1, 3)
+        gather_vector(2, 0, 2)
+        gather_vector(3, 0, 1)
+        gather_vector(3, 3, 4)
+
+        q_codes = sb.tile([P, Q], U32, name="q_codes", tag="key2", align_bytes=64)
         q_sc = sb.tile([P, Q], U8, name="q_sc", align_bytes=64)
         nc.vector.quantize_mx(out=q_codes[:].bitcast(FP8X4), scales=q_sc[:], in_=q_bf[:])
 
-        warm_bank = key_ps.tile([WARM_ROWS, T_HALF], F32, name="warm_bank", tag="key_bank")
-        for half in range(3):
-            nc.tensor.matmul_mx(
-                out=warm_bank[:],
-                lhsT=q_codes[:, :WARM_ROWS].bitcast(FP8X4),
-                lhsT_scale=q_sc[:, :WARM_ROWS],
-                rhs=emb_codes[half % 2][:].bitcast(FP8X4),
-                rhs_scale=emb_codes[half % 2][:].bitcast(U8)[:, :T_HALF],
-                start=True,
-                stop=True,
-            )
-
         woven = {}
-        for engine, first, last in WEAVES:
-            if engine == "vector":
-                tile = sb.tile([P, (last - first) * PACK], BF16, name="woven%d" % first, align_bytes=64)
-                nc.vector.tensor_copy(
-                    out=tile[:].rearrange("p (c i t) -> p c t i", i=4, t=PACK),
-                    in_=picked[:, :, first:last].rearrange("p t (c i) -> p c t i", i=4),
-                )
-                woven[first] = (tile, first)
-            else:
-                rows = slice(2, 4) if first == 0 else slice(1, 4, 2)
-                nc.scalar.copy(
-                    out=pairs[:, 1, first:last],
-                    in_=picked[:, rows, first:last].rearrange("p t i -> p i t"),
-                )
-                woven[first] = (ahead, 0)
-
-        early, late = slice(384, 512), slice(0, 384)
-        banks = [
-            key_ps.tile([P, early.stop - early.start], F32, name="scores_early", tag="key_bank"),
-            key_ps.tile([P, late.stop - late.start], F32, name="scores_late", tag="key_bank"),
-        ]
-        for first, last in PASSES:
-            tile, start = woven[first]
-            k_codes = sb.tile([P, last - first], U32, name="k_codes%d" % first, align_bytes=64)
-            k_sc = sb.tile([P, last - first], U8, name="k_sc%d" % first, align_bytes=64)
-            nc.vector.quantize_mx(
-                out=k_codes[:].bitcast(FP8X4),
-                scales=k_sc[:],
-                in_=tile[:, (first - start) * PACK : (last - start) * PACK],
+        for u in (0, 1):
+            slots = slice(u * I_QUARTER, (u + 1) * I_QUARTER)
+            nc.scalar.copy(out=pairs[:, 1, slots], in_=picked[:, 2:4, slots].rearrange("p t i -> p i t"))
+            woven[u] = ahead[:, u * I_QUARTER * PACK : (u + 1) * I_QUARTER * PACK]
+        for u in (3, 2):
+            tile = sb.tile([P, I_QUARTER * PACK], BF16, name="woven%d" % u, align_bytes=64)
+            nc.vector.tensor_copy(
+                out=tile[:].rearrange("p (c i t) -> p c t i", i=4, t=PACK),
+                in_=picked[:, :, u * I_QUARTER : (u + 1) * I_QUARTER].rearrange("p t (c i) -> p c t i", i=4),
             )
+            woven[u] = tile[:]
+
+        early = ps.tile([P, I_QUARTER], F32, name="scores_early", tag="bank")
+        late = ps.tile([P, I - I_QUARTER], F32, name="scores_late", tag="bank")
+        for u in PASSES:
+            k_codes = sb.tile([P, I_QUARTER], U32, name="k_codes%d" % u, align_bytes=64)
+            k_sc = sb.tile([P, I_QUARTER], U8, name="k_sc%d" % u, align_bytes=64)
+            nc.vector.quantize_mx(out=k_codes[:].bitcast(FP8X4), scales=k_sc[:], in_=woven[u])
             nc.tensor.matmul_mx(
-                out=(
-                    banks[0][:, first - early.start : last - early.start]
-                    if early.start <= first < early.stop
-                    else banks[1][:, first - late.start : last - late.start]
-                ),
+                out=early[:] if u == 3 else late[:, u * I_QUARTER : (u + 1) * I_QUARTER],
                 lhsT=q_codes[:].bitcast(FP8X4),
                 lhsT_scale=q_sc[:],
                 rhs=k_codes[:].bitcast(FP8X4),
@@ -238,7 +200,10 @@ def tile_attend_grouppick_fresh_kernel(tc, emb_words, emb_scales, wk, query, off
         neg = sb.tile([P, I], F32, name="neg")
         neg_max_early = sb.tile([P, 1], F32, name="neg_max_early")
         neg_max = sb.tile([P, 1], F32, name="neg_max")
-        for bank, part, start, result in ((banks[0], early, None, neg_max_early), (banks[1], late, neg_max_early[:], neg_max)):
+        for bank, part, start, result in (
+            (early, slice(I - I_QUARTER, I), None, neg_max_early),
+            (late, slice(0, I - I_QUARTER), neg_max_early[:], neg_max),
+        ):
             nc.vector.tensor_scalar(
                 out=neg[:, part],
                 in0=bank[:],
@@ -253,7 +218,6 @@ def tile_attend_grouppick_fresh_kernel(tc, emb_words, emb_scales, wk, query, off
         nc.scalar.activation(prob[:], neg[:], EXP, bias=neg_max[:], scale=-1.0, accum_out=total[:])
         inv = sb.tile([P, 1], F32, name="inv")
         nc.vector.reciprocal(inv[:], total[:])
-
         res = sb.tile([P, I], F32, name="res")
         nc.vector.tensor_scalar(
             out=res[:], in0=prob[:], scalar1=inv[:], scalar2=float(I), op0=ALU.mult, op1=ALU.mult

@@ -26,10 +26,13 @@ I_QUARTER = I // 4
 PLANE_CUTS = [
     [0, 256, 512, 640, 768, 896, 1024],
     [0, 256, 512, 768, 1024],
-    [0, 512, 1024],
-    [0, 512, 1024],
+    [0, 256, 512, 768, 1024],
+    [0, 256, 512, 768, 1024],
 ]
-SCALAR_COPIES = ((0, 256), (0, 512), (0, 640), (0, 768), (3, 512))
+VECTOR_COPIES = ((0, 0), (0, 512), (3, 768))
+WARM_TILE = (3, 512)
+WARM_ROWS = 32
+EARLY = 2
 PASSES = (3, 0, 2, 1)
 
 
@@ -115,7 +118,7 @@ def tile_attend_grouppick_fresh_kernel(tc, emb_words, emb_scales, wk, query, off
         for j in range(PACK):
             key = sb.tile([P, T], F32, name="key%d" % j, tag="key%d" % j, align_bytes=64)
             for first, last in zip(PLANE_CUTS[j], PLANE_CUTS[j][1:]):
-                bank = ps.tile([P, last - first], F32, name="bank")
+                bank = ps.tile([P, T_HALF], F32, name="bank")
                 starts = [first] + list(range(first // T_QUARTER * T_QUARTER + T_QUARTER, last, T_QUARTER))
                 for a, end in zip(starts, starts[1:] + [last]):
                     width = end - a
@@ -128,21 +131,33 @@ def tile_attend_grouppick_fresh_kernel(tc, emb_words, emb_scales, wk, query, off
                         start=True,
                         stop=True,
                     )
-                if (j, first) in SCALAR_COPIES:
-                    nc.scalar.copy(out=key[:, first:last], in_=bank[:])
+                if (j, first) in VECTOR_COPIES:
+                    nc.vector.tensor_copy(out=key[:, first:last], in_=bank[:, : last - first])
                 else:
-                    nc.vector.tensor_copy(out=key[:, first:last], in_=bank[:])
+                    nc.scalar.copy(out=key[:, first:last], in_=bank[:, : last - first])
+                if (j, first) == WARM_TILE:
+                    warm_bank = bank
             keys.append(key)
-            if j == 0:
-                gather_scalar(0, 0, 4)
-            if j == 1:
-                gather_scalar(1, 0, 4)
+
+        gather_vector(0, 0, 4)
+        gather_vector(1, 0, 4)
+
+        for n in range(3):
+            nc.tensor.matmul_mx(
+                out=warm_bank[:WARM_ROWS, :],
+                lhsT=wk_codes[3][:, :WARM_ROWS].bitcast(FP8X4),
+                lhsT_scale=wk_scales[3][:, :WARM_ROWS],
+                rhs=emb_codes[n % 2][:].bitcast(FP8X4),
+                rhs_scale=emb_codes[n % 2][:].bitcast(U8)[:, :T_HALF],
+                start=True,
+                stop=True,
+            )
 
         q_bf = sb.tile([P, Q * PACK], BF16, name="q_bf", align_bytes=64)
         nc.gpsimd.tensor_scalar(
             out=q_bf[:].rearrange("p (i t) -> p i t", t=PACK),
             in0=q_raw[:].rearrange("p (t i) -> p i t", t=PACK),
-            scalar1=1.0,
+            scalar1=-1.0,
             scalar2=0.0,
             op0=ALU.mult,
             op1=ALU.add,
@@ -181,38 +196,42 @@ def tile_attend_grouppick_fresh_kernel(tc, emb_words, emb_scales, wk, query, off
             )
             woven[u] = tile[:]
 
-        early = ps.tile([P, I_QUARTER], F32, name="scores_early", tag="bank")
-        late = ps.tile([P, I - I_QUARTER], F32, name="scores_late", tag="bank")
-        for u in PASSES:
+        neg = ps.tile([P, I], F32, name="neg", tag="bank")
+        early_banks = []
+        for n, u in enumerate(PASSES):
             k_codes = sb.tile([P, I_QUARTER], U32, name="k_codes%d" % u, align_bytes=64)
             k_sc = sb.tile([P, I_QUARTER], U8, name="k_sc%d" % u, align_bytes=64)
             nc.vector.quantize_mx(out=k_codes[:].bitcast(FP8X4), scales=k_sc[:], in_=woven[u])
-            nc.tensor.matmul_mx(
-                out=early[:] if u == 3 else late[:, u * I_QUARTER : (u + 1) * I_QUARTER],
-                lhsT=q_codes[:].bitcast(FP8X4),
-                lhsT_scale=q_sc[:],
-                rhs=k_codes[:].bitcast(FP8X4),
-                rhs_scale=k_sc[:],
-                start=True,
-                stop=True,
-            )
+            targets = [neg[:, u * I_QUARTER : (u + 1) * I_QUARTER]]
+            if n < EARLY:
+                own = ps.tile([P, I_QUARTER], F32, name="early%d" % n, tag="bank")
+                targets = [own[:]] + targets
+                early_banks.append(own)
+            for target in targets:
+                nc.tensor.matmul_mx(
+                    out=target,
+                    lhsT=q_codes[:].bitcast(FP8X4),
+                    lhsT_scale=q_sc[:],
+                    rhs=k_codes[:].bitcast(FP8X4),
+                    rhs_scale=k_sc[:],
+                    start=True,
+                    stop=True,
+                )
+        early_min = [sb.tile([P, 1], F32, name="early_min%d" % n) for n in range(EARLY)]
+        for least, own in zip(early_min, early_banks):
+            nc.vector.tensor_reduce(out=least[:], in_=own[:], axis=mybir.AxisListType.X, op=ALU.min)
 
-        neg = sb.tile([P, I], F32, name="neg")
-        neg_max_early = sb.tile([P, 1], F32, name="neg_max_early")
+        capped = sb.tile([P, 2 * I_QUARTER], F32, name="capped")
         neg_max = sb.tile([P, 1], F32, name="neg_max")
-        for bank, part, start, result in (
-            (early, slice(I - I_QUARTER, I), None, neg_max_early),
-            (late, slice(0, I - I_QUARTER), neg_max_early[:], neg_max),
-        ):
-            nc.vector.tensor_scalar(
-                out=neg[:, part],
-                in0=bank[:],
-                scalar1=-1.0,
-                scalar2=start,
-                op0=ALU.mult,
-                op1=ALU.min,
-                accum_out=result[:],
-            )
+        nc.vector.tensor_scalar(
+            out=capped[:],
+            in0=neg[:, I_QUARTER : 3 * I_QUARTER],
+            scalar1=early_min[0][:],
+            scalar2=early_min[1][:],
+            op0=ALU.min,
+            op1=ALU.min,
+            accum_out=neg_max[:],
+        )
         prob = sb.tile([P, I], F32, name="prob")
         total = sb.tile([P, 1], F32, name="total")
         nc.scalar.activation(prob[:], neg[:], EXP, bias=neg_max[:], scale=-1.0, accum_out=total[:])

@@ -43,13 +43,13 @@ def tile_attend_grouppick_fresh_kernel(tc, emb_words, emb_scales, wk, query, off
         ps = ctx.enter_context(tc.psum_pool(name="ps", bufs=8))
 
         offsets = sb.tile([P, I // LIST_ROWS], U16, name="offsets")
-        emb_sc = sb.tile([P, T_QUARTER], U8, name="emb_sc", align_bytes=64)
+        emb_sc = sb.tile([P, T_QUARTER], U8, name="emb_sc", align_bytes=256)
         nc.vector.memset(emb_sc[:].bitcast(I32), 0)
 
         wk_rows = wk.rearrange("(p t) d -> p t d", t=PACK)
         wk_raw = []
         for pair in range(2):
-            raw = sb.tile([P, 2, D], F32, name="wk_raw%d" % pair)
+            raw = sb.tile([P, 2, D], F32, name="wk_raw%d" % pair, align_bytes=256)
             nc.sync.dma_start(out=raw[:], in_=wk_rows[:, 2 * pair : 2 * pair + 2, :])
             wk_raw.append(raw)
         for g, queue in enumerate((nc.scalar, nc.scalar, nc.sync, nc.sync)):
@@ -60,14 +60,14 @@ def tile_attend_grouppick_fresh_kernel(tc, emb_words, emb_scales, wk, query, off
         emb_bytes = emb_words[0].rearrange("p n t -> p (n t)")
         emb_codes = []
         for half in range(2):
-            codes = sb.tile([P, T_HALF], U32, name="emb_codes%d" % half, align_bytes=64)
+            codes = sb.tile([P, T_HALF], U32, name="emb_codes%d" % half, align_bytes=256)
             nc.sync.dma_start(
                 out=codes[:].bitcast(I32),
                 in_=emb_bytes[:, half * T_HALF * PACK : (half + 1) * T_HALF * PACK].bitcast(I32),
             )
             emb_codes.append(codes)
         nc.sync.dma_start(offsets[:], offs)
-        q_raw = sb.tile([P, PACK * Q], F32, name="q_raw", align_bytes=64)
+        q_raw = sb.tile([P, PACK * Q], F32, name="q_raw", align_bytes=256)
         q_planes = query.rearrange("(b j r) q -> j b r q", j=PACK, r=8)
         for j in range(PACK):
             nc.sync.dma_start(out=q_raw[:, j * Q : (j + 1) * Q], in_=q_planes[j])
@@ -162,7 +162,7 @@ def tile_attend_grouppick_fresh_kernel(tc, emb_words, emb_scales, wk, query, off
             op0=ALU.mult,
             op1=ALU.add,
         )
-        ahead = sb.tile([P, 2 * I_QUARTER * PACK], BF16, name="ahead", tag="q_raw", align_bytes=64)
+        ahead = sb.tile([P, 2 * I_QUARTER * PACK], BF16, name="ahead", tag="q_raw", align_bytes=256)
         pairs = ahead[:].rearrange("p (i c t) -> p c i t", c=2, t=2)
         nc.gpsimd.tensor_scalar(
             out=pairs[:, 0],
@@ -237,7 +237,7 @@ def tile_attend_grouppick_fresh_kernel(tc, emb_words, emb_scales, wk, query, off
         nc.scalar.activation(prob[:], neg[:], EXP, bias=neg_max[:], scale=-1.0, accum_out=total[:])
         inv = sb.tile([P, 1], F32, name="inv")
         nc.vector.reciprocal(inv[:], total[:])
-        res = sb.tile([P, I], F32, name="res")
+        res = sb.tile([P, I], F32, name="res", align_bytes=256)
         nc.vector.tensor_scalar(
             out=res[:], in0=prob[:], scalar1=inv[:], scalar2=float(I), op0=ALU.mult, op1=ALU.mult
         )

@@ -74,7 +74,7 @@ def tile_attend_grouppick_fresh_kernel(tc, emb_words, emb_scales, wk, query, off
 
         parts = [(0, 0, P // 2), (0, P // 2, P)] + [(j, 0, P) for j in range(1, PACK)]
         wk_bf = [
-            sb.tile([P, (last - first) * PACK], BF16, name="wk_bf%d_%d" % (j, first), align_bytes=64)
+            sb.tile([P, (last - first) * PACK], BF16, name="wk_bf%d_%d" % (j, first), align_bytes=256)
             for j, first, last in parts
         ]
         for pair in range(2):
@@ -90,15 +90,15 @@ def tile_attend_grouppick_fresh_kernel(tc, emb_words, emb_scales, wk, query, off
                     nc.scalar.copy(out=dst, in_=rows)
 
         wk_codes = [
-            sb.tile([P, P], U32, name="wk_codes%d" % j, tag="stationary%d" % j, align_bytes=64) for j in range(PACK)
+            sb.tile([P, P], U32, name="wk_codes%d" % j, tag="stationary%d" % j, align_bytes=256) for j in range(PACK)
         ]
-        wk_scales = [sb.tile([P, P], U8, name="wk_sc%d" % j, align_bytes=64) for j in range(PACK)]
+        wk_scales = [sb.tile([P, P], U8, name="wk_sc%d" % j, align_bytes=256) for j in range(PACK)]
         for tile, (j, first, last) in zip(wk_bf, parts):
             nc.vector.quantize_mx(
                 out=wk_codes[j][:, first:last].bitcast(FP8X4), scales=wk_scales[j][:, first:last], in_=tile[:]
             )
 
-        picked = sb.tile([P, PACK, I], F32, name="picked")
+        picked = sb.tile([P, PACK, I], F32, name="picked", align_bytes=256)
         quarter = I_QUARTER // LIST_ROWS
         keys = []
 
@@ -116,7 +116,7 @@ def tile_attend_grouppick_fresh_kernel(tc, emb_words, emb_scales, wk, query, off
             )
 
         for j in range(PACK):
-            key = sb.tile([P, T], F32, name="key%d" % j, tag="key%d" % j, align_bytes=64)
+            key = sb.tile([P, T], F32, name="key%d" % j, tag="key%d" % j, align_bytes=256)
             for first, last in zip(PLANE_CUTS[j], PLANE_CUTS[j][1:]):
                 bank = ps.tile([P, T_HALF], F32, name="bank")
                 starts = [first] + list(range(first // T_QUARTER * T_QUARTER + T_QUARTER, last, T_QUARTER))
@@ -153,7 +153,7 @@ def tile_attend_grouppick_fresh_kernel(tc, emb_words, emb_scales, wk, query, off
                 stop=True,
             )
 
-        q_bf = sb.tile([P, Q * PACK], BF16, name="q_bf", align_bytes=64)
+        q_bf = sb.tile([P, Q * PACK], BF16, name="q_bf", align_bytes=256)
         nc.gpsimd.tensor_scalar(
             out=q_bf[:].rearrange("p (i t) -> p i t", t=PACK),
             in0=q_raw[:].rearrange("p (t i) -> p i t", t=PACK),
@@ -179,8 +179,8 @@ def tile_attend_grouppick_fresh_kernel(tc, emb_words, emb_scales, wk, query, off
         gather_vector(3, 0, 1)
         gather_vector(3, 3, 4)
 
-        q_codes = sb.tile([P, Q], U32, name="q_codes", tag="key2", align_bytes=64)
-        q_sc = sb.tile([P, Q], U8, name="q_sc", align_bytes=64)
+        q_codes = sb.tile([P, Q], U32, name="q_codes", tag="key2", align_bytes=256)
+        q_sc = sb.tile([P, Q], U8, name="q_sc", align_bytes=256)
         nc.vector.quantize_mx(out=q_codes[:].bitcast(FP8X4), scales=q_sc[:], in_=q_bf[:])
 
         woven = {}
@@ -189,7 +189,7 @@ def tile_attend_grouppick_fresh_kernel(tc, emb_words, emb_scales, wk, query, off
             nc.scalar.copy(out=pairs[:, 1, slots], in_=picked[:, 2:4, slots].rearrange("p t i -> p i t"))
             woven[u] = ahead[:, u * I_QUARTER * PACK : (u + 1) * I_QUARTER * PACK]
         for u in (3, 2):
-            tile = sb.tile([P, I_QUARTER * PACK], BF16, name="woven%d" % u, align_bytes=64)
+            tile = sb.tile([P, I_QUARTER * PACK], BF16, name="woven%d" % u, align_bytes=256)
             nc.vector.tensor_copy(
                 out=tile[:].rearrange("p (c i t) -> p c t i", i=4, t=PACK),
                 in_=picked[:, :, u * I_QUARTER : (u + 1) * I_QUARTER].rearrange("p t (c i) -> p c t i", i=4),
@@ -199,8 +199,8 @@ def tile_attend_grouppick_fresh_kernel(tc, emb_words, emb_scales, wk, query, off
         neg = ps.tile([P, I], F32, name="neg", tag="bank")
         early_banks = []
         for n, u in enumerate(PASSES):
-            k_codes = sb.tile([P, I_QUARTER], U32, name="k_codes%d" % u, align_bytes=64)
-            k_sc = sb.tile([P, I_QUARTER], U8, name="k_sc%d" % u, align_bytes=64)
+            k_codes = sb.tile([P, I_QUARTER], U32, name="k_codes%d" % u, align_bytes=256)
+            k_sc = sb.tile([P, I_QUARTER], U8, name="k_sc%d" % u, align_bytes=256)
             nc.vector.quantize_mx(out=k_codes[:].bitcast(FP8X4), scales=k_sc[:], in_=woven[u])
             targets = [neg[:, u * I_QUARTER : (u + 1) * I_QUARTER]]
             if n < EARLY:
@@ -221,7 +221,7 @@ def tile_attend_grouppick_fresh_kernel(tc, emb_words, emb_scales, wk, query, off
         for least, own in zip(early_min, early_banks):
             nc.vector.tensor_reduce(out=least[:], in_=own[:], axis=mybir.AxisListType.X, op=ALU.min)
 
-        capped = sb.tile([P, 2 * I_QUARTER], F32, name="capped")
+        capped = sb.tile([P, 2 * I_QUARTER], F32, name="capped", align_bytes=256)
         neg_max = sb.tile([P, 1], F32, name="neg_max")
         nc.vector.tensor_scalar(
             out=capped[:],
@@ -232,7 +232,7 @@ def tile_attend_grouppick_fresh_kernel(tc, emb_words, emb_scales, wk, query, off
             op1=ALU.min,
             accum_out=neg_max[:],
         )
-        prob = sb.tile([P, I], F32, name="prob")
+        prob = sb.tile([P, I], F32, name="prob", align_bytes=256)
         total = sb.tile([P, 1], F32, name="total")
         nc.scalar.activation(prob[:], neg[:], EXP, bias=neg_max[:], scale=-1.0, accum_out=total[:])
         inv = sb.tile([P, 1], F32, name="inv")

@@ -52,7 +52,7 @@ def tile_attend_grouppick_fresh_kernel(tc, emb_words, emb_scales, wk, query, off
             raw = sb.tile([P, 2, D], F32, name="wk_raw%d" % pair, align_bytes=256)
             nc.sync.dma_start(out=raw[:], in_=wk_rows[:, 2 * pair : 2 * pair + 2, :])
             wk_raw.append(raw)
-        for g, queue in enumerate((nc.scalar, nc.scalar, nc.sync, nc.sync)):
+        for g, queue in enumerate((nc.sync, nc.sync, nc.sync, nc.sync)):
             queue.dma_start(
                 out=emb_sc[32 * g : 32 * g + 16, :].bitcast(I32),
                 in_=emb_scales[0, 4 * g : 4 * g + 4, :].bitcast(I32).rearrange("r (c n) -> c r n", c=4),

from contextlib import ExitStack

import concourse.mybir as mybir

K, T, D, I, Q = 512, 1024, 512, 512, 128
FLOPS = 2 * K * D * T + 2 * D * Q * I

F32 = mybir.dt.float32
BF16 = mybir.dt.bfloat16
I32 = mybir.dt.int32
U32 = mybir.dt.uint32
U16 = mybir.dt.uint16
U8 = mybir.dt.uint8
FP8X4 = mybir.dt.float8_e4m3fn_x4
ALU = mybir.AluOpType
EXP = mybir.ActivationFunctionType.Exp
COPY = mybir.ActivationFunctionType.Copy

P = 128
PACK = 4
LIST_ROWS = 16
T_HALF = T // 2
T_QUARTER = T // 4
I_QUARTER = I // 4

PLANE_CUTS = [
    [0, 256, 512, 640, 768, 896, 1024],
    [0, 256, 512, 768, 1024],
    [0, 256, 512, 768, 1024],
    [0, 256, 512, 768, 1024],
]
VECTOR_COPIES = ((0, 0), (0, 512), (3, 768))
WARM_TILE = (3, 512)
WARM_ROWS = 32
EARLY = 2
PASSES = (3, 0, 2, 1)


def tile_attend_grouppick_fresh_kernel(tc, emb_words, emb_scales, wk, query, offs, out):
    nc = tc.nc
    with ExitStack() as ctx:
        sb = ctx.enter_context(tc.tile_pool(name="sb", bufs=1))
        ps = ctx.enter_context(tc.psum_pool(name="ps", bufs=8))

        offsets = sb.tile([P, I // LIST_ROWS], U16, name="offsets")
        emb_sc = sb.tile([P, T_QUARTER], U8, name="emb_sc", align_bytes=256)
        nc.vector.memset(emb_sc[:].bitcast(I32), 0)

        wk_rows = wk.rearrange("(p t) d -> p t d", t=PACK)
        wk_raw = []
        for pair in range(2):
            raw = sb.tile([P, 2, D], F32, name="wk_raw%d" % pair, align_bytes=256)
            nc.sync.dma_start(out=raw[:], in_=wk_rows[:, 2 * pair : 2 * pair + 2, :])
            wk_raw.append(raw)
        for g, queue in enumerate((nc.sync, nc.sync, nc.sync, nc.sync)):
            queue.dma_start(
                out=emb_sc[32 * g : 32 * g + 16, :].bitcast(I32),
                in_=emb_scales[0, 4 * g : 4 * g + 4, :].bitcast(I32).rearrange("r (c n) -> c r n", c=4),
            )
        emb_bytes = emb_words[0].rearrange("p n t -> p (n t)")
        emb_codes = []
        for half in range(2):
            codes = sb.tile([P, T_HALF], U32, name="emb_codes%d" % half, align_bytes=256)
            nc.sync.dma_start(
                out=codes[:].bitcast(I32),
                in_=emb_bytes[:, half * T_HALF * PACK : (half + 1) * T_HALF * PACK].bitcast(I32),
            )
            emb_codes.append(codes)
        nc.sync.dma_start(offsets[:], offs)
        q_raw = sb.tile([P, PACK * Q], F32, name="q_raw", align_bytes=256)
        q_planes = query.rearrange("(b j r) q -> j b r q", j=PACK, r=8)
        for j in range(PACK):
            nc.sync.dma_start(out=q_raw[:, j * Q : (j + 1) * Q], in_=q_planes[j])

        parts = [(0, 0, P // 2), (0, P // 2, P)] + [(j, 0, P) for j in range(1, PACK)]
        wk_bf = [
            sb.tile([P, (last - first) * PACK], BF16, name="wk_bf%d_%d" % (j, first), align_bytes=256)
            for j, first, last in parts
        ]
        for pair in range(2):
            src = wk_raw[pair][:].rearrange("p t (b j r) -> p j b r t", j=PACK, r=8)
            for tile, (j, first, last) in zip(wk_bf, parts):
                dst = tile[:].rearrange("p (b r c t) -> p c b r t", c=2, r=8, t=2)[:, pair]
                rows = src[:, j, first // 8 : last // 8]
                if j == 0 or (j == 1 and pair == 0):
                    nc.vector.tensor_copy(out=dst, in_=rows)
                elif pair == 0:
                    nc.scalar.activation(dst, rows, COPY)
                else:
                    nc.scalar.copy(out=dst, in_=rows)

        wk_codes = [
            sb.tile([P, P], U32, name="wk_codes%d" % j, tag="stationary%d" % j, align_bytes=256) for j in range(PACK)
        ]
        wk_scales = [sb.tile([P, P], U8, name="wk_sc%d" % j, align_bytes=256) for j in range(PACK)]
        for tile, (j, first, last) in zip(wk_bf, parts):
            nc.vector.quantize_mx(
                out=wk_codes[j][:, first:last].bitcast(FP8X4), scales=wk_scales[j][:, first:last], in_=tile[:]
            )

        picked = sb.tile([P, PACK, I], F32, name="picked", align_bytes=256)
        quarter = I_QUARTER // LIST_ROWS
        keys = []

        def gather_scalar(j, first, last):
            nc.scalar.activation(
                picked[:, j, first * I_QUARTER : last * I_QUARTER],
                keys[j][:].indirect(offsets[:, first * quarter : last * quarter]),
                COPY,
            )

        def gather_vector(j, first, last):
            nc.vector.tensor_copy(
                out=picked[:, j, first * I_QUARTER : last * I_QUARTER].bitcast(U32),
                in_=keys[j][:].bitcast(U32).indirect(offsets[:, first * quarter : last * quarter]),
            )

        for j in range(PACK):
            key = sb.tile([P, T], F32, name="key%d" % j, tag="key%d" % j, align_bytes=256)
            for first, last in zip(PLANE_CUTS[j], PLANE_CUTS[j][1:]):
                bank = ps.tile([P, T_HALF], F32, name="bank")
                starts = [first] + list(range(first // T_QUARTER * T_QUARTER + T_QUARTER, last, T_QUARTER))
                for a, end in zip(starts, starts[1:] + [last]):
                    width = end - a
                    nc.tensor.matmul_mx(
                        out=bank[:, a - first : a - first + width],
                        lhsT=wk_codes[j][:].bitcast(FP8X4),
                        lhsT_scale=wk_scales[j][:],
                        rhs=emb_codes[a // T_HALF][:, a % T_HALF : a % T_HALF + width].bitcast(FP8X4),
                        rhs_scale=emb_sc[4 * (a // T_QUARTER) :, a % T_QUARTER : a % T_QUARTER + width],
                        start=True,
                        stop=True,
                    )
                if (j, first) in VECTOR_COPIES:
                    nc.vector.tensor_copy(out=key[:, first:last], in_=bank[:, : last - first])
                else:
                    nc.scalar.copy(out=key[:, first:last], in_=bank[:, : last - first])
                if (j, first) == WARM_TILE:
                    warm_bank = bank
            keys.append(key)

        gather_vector(0, 0, 4)
        gather_vector(1, 0, 4)

        for n in range(3):
            nc.tensor.matmul_mx(
                out=warm_bank[:WARM_ROWS, :],
                lhsT=wk_codes[3][:, :WARM_ROWS].bitcast(FP8X4),
                lhsT_scale=wk_scales[3][:, :WARM_ROWS],
                rhs=emb_codes[n % 2][:].bitcast(FP8X4),
                rhs_scale=emb_codes[n % 2][:].bitcast(U8)[:, :T_HALF],
                start=True,
                stop=True,
            )

        q_bf = sb.tile([P, Q * PACK], BF16, name="q_bf", align_bytes=256)
        nc.gpsimd.tensor_scalar(
            out=q_bf[:].rearrange("p (i t) -> p i t", t=PACK),
            in0=q_raw[:].rearrange("p (t i) -> p i t", t=PACK),
            scalar1=-1.0,
            scalar2=0.0,
            op0=ALU.mult,
            op1=ALU.add,
        )
        ahead = sb.tile([P, 2 * I_QUARTER * PACK], BF16, name="ahead", tag="q_raw", align_bytes=256)
        pairs = ahead[:].rearrange("p (i c t) -> p c i t", c=2, t=2)
        nc.gpsimd.tensor_scalar(
            out=pairs[:, 0],
            in0=picked[:, 0:2, : 2 * I_QUARTER].rearrange("p t i -> p i t"),
            scalar1=1.0,
            scalar2=0.0,
            op0=ALU.mult,
            op1=ALU.add,
        )

        gather_scalar(2, 2, 4)
        gather_scalar(3, 1, 3)
        gather_vector(2, 0, 2)
        gather_vector(3, 0, 1)
        gather_vector(3, 3, 4)

        q_codes = sb.tile([P, Q], U32, name="q_codes", tag="key2", align_bytes=256)
        q_sc = sb.tile([P, Q], U8, name="q_sc", align_bytes=256)
        nc.vector.quantize_mx(out=q_codes[:].bitcast(FP8X4), scales=q_sc[:], in_=q_bf[:])

        woven = {}
        for u in (0, 1):
            slots = slice(u * I_QUARTER, (u + 1) * I_QUARTER)
            nc.scalar.copy(out=pairs[:, 1, slots], in_=picked[:, 2:4, slots].rearrange("p t i -> p i t"))
            woven[u] = ahead[:, u * I_QUARTER * PACK : (u + 1) * I_QUARTER * PACK]
        for u in (3, 2):
            tile = sb.tile([P, I_QUARTER * PACK], BF16, name="woven%d" % u, align_bytes=256)
            nc.vector.tensor_copy(
                out=tile[:].rearrange("p (c i t) -> p c t i", i=4, t=PACK),
                in_=picked[:, :, u * I_QUARTER : (u + 1) * I_QUARTER].rearrange("p t (c i) -> p c t i", i=4),
            )
            woven[u] = tile[:]

        neg = ps.tile([P, I], F32, name="neg", tag="bank")
        early_banks = []
        for n, u in enumerate(PASSES):
            k_codes = sb.tile([P, I_QUARTER], U32, name="k_codes%d" % u, align_bytes=256)
            k_sc = sb.tile([P, I_QUARTER], U8, name="k_sc%d" % u, align_bytes=256)
            nc.vector.quantize_mx(out=k_codes[:].bitcast(FP8X4), scales=k_sc[:], in_=woven[u])
            targets = [neg[:, u * I_QUARTER : (u + 1) * I_QUARTER]]
            if n < EARLY:
                own = ps.tile([P, I_QUARTER], F32, name="early%d" % n, tag="bank")
                targets = [own[:]] + targets
                early_banks.append(own)
            for target in targets:
                nc.tensor.matmul_mx(
                    out=target,
                    lhsT=q_codes[:].bitcast(FP8X4),
                    lhsT_scale=q_sc[:],
                    rhs=k_codes[:].bitcast(FP8X4),
                    rhs_scale=k_sc[:],
                    start=True,
                    stop=True,
                )
        early_min = [sb.tile([P, 1], F32, name="early_min%d" % n) for n in range(EARLY)]
        for least, own in zip(early_min, early_banks):
            nc.vector.tensor_reduce(out=least[:], in_=own[:], axis=mybir.AxisListType.X, op=ALU.min)

        capped = sb.tile([P, 2 * I_QUARTER], F32, name="capped", align_bytes=256)
        neg_max = sb.tile([P, 1], F32, name="neg_max")
        nc.vector.tensor_scalar(
            out=capped[:],
            in0=neg[:, I_QUARTER : 3 * I_QUARTER],
            scalar1=early_min[0][:],
            scalar2=early_min[1][:],
            op0=ALU.min,
            op1=ALU.min,
            accum_out=neg_max[:],
        )
        prob = sb.tile([P, I], F32, name="prob", align_bytes=256)
        total = sb.tile([P, 1], F32, name="total")
        nc.scalar.activation(prob[:], neg[:], EXP, bias=neg_max[:], scale=-1.0, accum_out=total[:])
        inv = sb.tile([P, 1], F32, name="inv")
        nc.vector.reciprocal(inv[:], total[:])
        res = sb.tile([P, I], F32, name="res", align_bytes=256)
        nc.vector.tensor_scalar(
            out=res[:], in0=prob[:], scalar1=inv[:], scalar2=float(I), op0=ALU.mult, op1=ALU.mult
        )
        nc.sync.dma_start(out=out, in_=res[:])
